import numpy as np
import ml_dtypes


def mxq(x, axis, fmt="e4m3"):
    dtype, down = {"e4m3": (ml_dtypes.float8_e4m3fn, 7), "e5m2": (ml_dtypes.float8_e5m2, 14)}[fmt]
    v = np.moveaxis(np.asarray(x, np.float32).astype(ml_dtypes.bfloat16).astype(np.float64), axis, -1)
    blocks = v.reshape(v.shape[:-1] + (-1, 32))
    amax = np.abs(blocks).max(-1, keepdims=True)
    byte = np.maximum(np.where(amax > 0, np.frexp(amax)[1] - 1 + 127, 0) - down, 1)
    scale = np.exp2(byte - 127.0)
    codes = (blocks / scale).astype(np.float32).astype(dtype).astype(np.float64)
    return np.moveaxis((codes * scale).reshape(v.shape), -1, axis)


WIDE = False


def mx_kscale(k):
    if not WIDE:
        return np.ones(k)
    levels = np.array([10, -10, 5, -5, 0])
    if k % 512:
        return np.exp2(np.random.permutation(np.resize(levels, k // 32))).repeat(32)
    a = np.empty((k // 512, 16))
    for p in range(k // 512):
        a[p, :8] = np.random.permutation(np.resize(levels, 8))
        for g in range(8):
            far = levels[np.abs(levels - a[p, g]) >= 10]
            a[p, g + 8] = far[np.random.randint(len(far))]
    return np.exp2(a.ravel()).repeat(32)


BF16 = ml_dtypes.bfloat16


def bf(x):
    return np.asarray(x, np.float32).astype(BF16)


def f64(x):
    return np.asarray(x).astype(np.float64)


E2M1 = np.array([0.0, 0.5, 1.0, 1.5, 2.0, 3.0, 4.0, 6.0, -0.0, -0.5, -1.0, -1.5, -2.0, -3.0, -4.0, -6.0])


def pack_weight(w, fmt):
    k, n = w.shape
    w = f64(bf(w)).reshape(k // 32, 32, n)
    amax = np.abs(w).max(1)
    if fmt == "e4m3":
        byte = np.frexp(amax)[1] - 1 + 127 - 7
    else:
        mant, ex = np.frexp(amax / 6.0)
        byte = np.where(mant > 0.5, ex, ex - 1) + 127
    byte = np.clip(np.where(amax > 0, byte, 1), 1, 254)
    scaled = (w * np.exp2(127.0 - byte)[:, None, :]).reshape(k, n).astype(np.float32)
    by_word = np.ascontiguousarray(scaled.reshape(k // 512, 128, 4, n).transpose(0, 1, 3, 2))
    if fmt == "e4m3":
        words = by_word.astype(ml_dtypes.float8_e4m3fn).view(np.uint8)
    else:
        c = by_word.astype(ml_dtypes.float4_e2m1fn).view(np.uint8) & 0xF
        words = c[..., 0::2] | (c[..., 1::2] << 4)
    return np.ascontiguousarray(words), np.ascontiguousarray(byte.astype(np.uint8).reshape(k // 512, 16, n))


def unpack_weight(words, scales, fmt):
    g, p, n, _ = words.shape
    if fmt == "e4m3":
        vals = np.ascontiguousarray(words).view(ml_dtypes.float8_e4m3fn).astype(np.float64)
    else:
        nib = np.empty((g, p, n, 4), np.uint8)
        nib[..., 0::2] = words & 0xF
        nib[..., 1::2] = words >> 4
        vals = E2M1[nib]
    vals = vals * np.repeat(np.exp2(scales.astype(np.float64) - 127.0), 8, axis=1)[..., None]
    return vals.transpose(0, 1, 3, 2).reshape(g * 512, n)

def planes(Y):
    n, m = Y.shape
    b = f64(bf(Y)).reshape(n // 32, 32, m)
    amax = np.abs(b).max(1)
    byte = np.clip(np.where(amax > 0, np.frexp(amax)[1] - 1 + 127 - 7, 1), 1, 254)
    codes = (b * np.exp2(127.0 - byte)[:, None, :]).reshape(n, m).astype(np.float32).astype(ml_dtypes.float8_e4m3fn).view(np.uint8)
    words = codes.reshape(n // 512, 128, 4, m).transpose(0, 1, 3, 2)
    return np.ascontiguousarray(words), np.ascontiguousarray(byte.astype(np.uint8).reshape(n // 512, 16, m))


F, K, T, TAU = 512, 512, 1024, 4
TK = TAU * K
TF = TAU * F


def softplus(a):
    return np.maximum(a, 0.0) + np.log1p(np.exp(-np.abs(a)))


def delay(x, tau):
    n = x.shape[1]
    return np.concatenate([x[:, n - tau:], x[:, :n - tau]], axis=1)


def advance(x, tau):
    return np.concatenate([x[:, tau:], x[:, :tau]], axis=1)


def setup_inputs():
    s, u = mx_kscale(TK), mx_kscale(TF)
    v = bf(np.random.uniform(0.2, 1.8, (F, T)))
    h = bf(np.random.uniform(0.2, 1.8, (K, T)))
    w1 = np.random.standard_normal((F, TK)) / np.sqrt(TK) / s[None, :]
    w1_words, w1_scales = pack_weight(w1.T, "e4m3")
    g1 = bf(np.random.standard_normal(TK) * s)
    w2 = np.random.standard_normal((K, TF)) * 1.5 / np.sqrt(TF) / u[None, :]
    w2_words, w2_scales = pack_weight(w2.T, "e4m3")
    g2 = bf((1.0 + 0.2 * np.random.standard_normal(TF)) * u)
    mu = bf(np.random.uniform(0.1, 0.5, K))
    return {
        "v": v,
        "h": h,
        "w1_words": w1_words,
        "w1_scales": w1_scales,
        "g1": g1,
        "w2_words": w2_words,
        "w2_scales": w2_scales,
        "g2": g2,
        "mu": mu,
    }


def core(v, h, w1_words, w1_scales, g1, w2_words, w2_scales, g2, mu):
    v, h, g1, g2, mu = f64(v), f64(h), f64(g1), f64(g2), f64(mu)
    w1 = unpack_weight(w1_words, w1_scales, "e4m3").T
    w2 = unpack_weight(w2_words, w2_scales, "e4m3").T
    hs = np.concatenate([delay(h, tau) for tau in range(TAU)], axis=0)
    hg = g1[:, None] * hs
    s = w1 @ mxq(hg, 0, "e4m3")
    e = v / (softplus(s) + 0.25) - 1.0
    es = np.concatenate([advance(e, tau) for tau in range(TAU)], axis=0)
    eg = g2[:, None] * es
    r = w2 @ mxq(eg, 0, "e4m3")
    return h * np.exp(0.5 * (r - mu[:, None]))


def reference(v, h, w1_words, w1_scales, g1, w2_words, w2_scales, g2, mu):
    R_out = core(v, h, w1_words, w1_scales, g1, w2_words, w2_scales, g2, mu)
    words, scales = planes(R_out.T)
    return R_out, words, scales

@@ -1,0 +1,388 @@
+from contextlib import ExitStack
+
+import concourse.mybir as mybir
+from concourse.masks import make_identity
+
+F32 = mybir.dt.float32
+BF16 = mybir.dt.bfloat16
+I32 = mybir.dt.int32
+U32 = mybir.dt.uint32
+U8 = mybir.dt.uint8
+FP8X4 = mybir.dt.float8_e4m3fn_x4
+ACT = mybir.ActivationFunctionType
+ALU = mybir.AluOpType
+
+P = 128
+TAPS = 4
+PACK = 4
+T = 1024
+HALF = 512
+FLOPS = 2 * 2 * 512 * 2048 * 1024
+EXP_QUARTER = 1.2840254166877414
+
+
+def tile_convolutivenmfexponentiatedupdate_x2_kernel(
+    tc, v, h, w1_words, w1_scales, g1, w2_words, w2_scales, g2, mu, out_0, out_1, out_2
+):
+    nc = tc.nc
+    with ExitStack() as ctx:
+        keep = ctx.enter_context(tc.tile_pool(name="keep", bufs=1))
+        work = ctx.enter_context(tc.tile_pool(name="work", bufs=3))
+        psum = ctx.enter_context(tc.psum_pool(name="psum", bufs=8))
+        ctx.enter_context(tc.manual_schedule())
+
+        warm = keep.tile([P, 1], F32, name="warm")
+        g1_t = keep.tile([P, TAPS, PACK], BF16, name="g1_t")
+        g2_t = keep.tile([P, TAPS, PACK], BF16, name="g2_t")
+        mu_t = keep.tile([P, 4, 2], BF16, name="mu_t")
+        mu_b = keep.tile([P, 4], F32, name="mu_b")
+        h_tail = keep.tile([P, PACK, 4], BF16, name="h_tail")
+        h_raw = keep.tile([P, PACK, T], BF16, name="h_raw")
+        h_int = keep.tile([P, 3 + T, PACK], BF16, name="h_int")
+        h_nat = keep.tile([P, 4, T], BF16, name="h_nat")
+        v_raw = keep.tile([P, PACK, T], BF16, name="v_raw")
+        v_int = keep.tile([P, T, PACK], BF16, name="v_int")
+        w1w_raw = keep.tile([P, TAPS, 512], I32, name="w1w_raw")
+        w1w = keep.tile([P, TAPS, PACK, P], I32, name="w1w", align_bytes=64)
+        w1s_raw = keep.tile([P, 512], U8, name="w1s_raw", align_bytes=64)
+        w1s = keep.tile([P, PACK, P], U8, name="w1s", align_bytes=64)
+        w2w = keep.tile([P, TAPS, 512], I32, name="w2w", align_bytes=64)
+        w2s = keep.tile([P, 512], U8, name="w2s", align_bytes=64)
+        ident = keep.tile([P, P], F32, name="ident")
+        lg = keep.tile([P, PACK, T], F32, name="lg")
+        e_int = keep.tile([P, T + 3, PACK], F32, name="e_int")
+
+        nc.vector.memset(warm[:], 0.0)
+        nc.scalar.activation(out=warm[:], in_=warm[:], func=ACT.Exp)
+        nc.vector.memset(w1s_raw[:].bitcast(I32), 0)
+        nc.gpsimd.memset(w2s[:].bitcast(I32), 0)
+        make_identity(nc, ident[:])
+
+        h_pj = h.rearrange("(p j) t -> p j t", j=PACK)
+        v_pj = v.rearrange("(p j) t -> p j t", j=PACK)
+        nc.sync.dma_start(out=g1_t[:], in_=g1.rearrange("(u p j) -> p u j", u=TAPS, j=PACK))
+        nc.sync.dma_start(out=h_tail[:], in_=h_pj[:, :, T - 4 : T])
+        nc.sync.dma_start(out=h_raw[:, :, 0:HALF], in_=h_pj[:, :, 0:HALF])
+        nc.sync.dma_start(out=h_raw[:, :, HALF:T], in_=h_pj[:, :, HALF:T])
+        nc.sync.dma_start(out=v_raw[:, :, 0:HALF], in_=v_pj[:, :, 0:HALF])
+        for q in range(4):
+            nc.sync.dma_start(
+                out=w1s_raw[32 * q : 32 * q + 16, :].bitcast(I32),
+                in_=w1_scales[:, 4 * q : 4 * q + 4, :].bitcast(I32),
+            )
+        for u in range(TAPS):
+            nc.sync.dma_start(
+                out=w1w_raw[:, u, :], in_=w1_words[u].rearrange("p n b -> p (n b)").bitcast(I32)
+            )
+        nc.gpsimd.dma_start(out=g2_t[:], in_=g2.rearrange("(u p j) -> p u j", u=TAPS, j=PACK))
+        nc.gpsimd.dma_start(
+            out=mu_t[:, :, 0:1], in_=mu.rearrange("(m p o) -> p m o", m=4, o=1)
+        )
+        nc.sync.dma_start(out=v_raw[:, :, HALF:T], in_=v_pj[:, :, HALF:T])
+        for q in range(4):
+            nc.sync.dma_start(
+                out=w2s[32 * q : 32 * q + 16, :].bitcast(I32),
+                in_=w2_scales[:, 4 * q : 4 * q + 4, :].bitcast(I32),
+            )
+        for u in range(TAPS):
+            nc.sync.dma_start(
+                out=w2w[:, u, :], in_=w2_words[u].rearrange("p n b -> p (n b)").bitcast(I32)
+            )
+        nc.sync.dma_start(out=h_nat[:], in_=h.rearrange("(m p) t -> p m t", p=P))
+
+        def lay(engine_copy, dst, dst0, src, a, b):
+            engine_copy(
+                out=dst[:, dst0 : dst0 + b - a, :], in_=src[:, :, a:b].rearrange("p j c -> p c j")
+            )
+
+        def gain1(half, u):
+            hg = work.tile([P, HALF, PACK], BF16, name="hg", align_bytes=64)
+            c0 = half * HALF + 3 - u
+            nc.vector.tensor_tensor(
+                out=hg[:],
+                in0=h_int[:, c0 : c0 + HALF, :],
+                in1=g1_t[:, u, :].unsqueeze(1).to_broadcast([P, HALF, PACK]),
+                op=ALU.mult,
+            )
+            return hg
+
+        def quant(src, width, name):
+            codes = work.tile([P, HALF], U32, name=name + "_c", align_bytes=64, bufs=6)
+            scales = work.tile([P, HALF], U8, name=name + "_s", align_bytes=64, bufs=6)
+            nc.vector.quantize_mx(
+                out=codes[:, 0:width].bitcast(FP8X4),
+                scales=scales[:, 0:width],
+                in_=src[:, 0:width, :].rearrange("p c j -> p (c j)"),
+            )
+            return codes, scales
+
+        def mm1(banks, u, q):
+            for j in range(PACK):
+                nc.tensor.matmul_mx(
+                    out=banks[j][:],
+                    lhsT=w1w[:, u, j, :].bitcast(FP8X4),
+                    lhsT_scale=w1s[4 * u : P, j, :],
+                    rhs=q[0][:].bitcast(FP8X4),
+                    rhs_scale=q[1][:],
+                    start=(u == 0),
+                    stop=(u == TAPS - 1),
+                )
+
+        def permute_words(u):
+            nc.vector.tensor_copy(
+                out=w1w[:, u, :, :], in_=w1w_raw[:, u, :].rearrange("p (m j) -> p j m", j=PACK)
+            )
+
+        def permute_scales():
+            nc.vector.tensor_copy(
+                out=w1s[:].rearrange("p j m -> p m j"),
+                in_=w1s_raw[:].rearrange("p (m j) -> p m j", j=PACK),
+            )
+
+        def banks_of(tag):
+            got = []
+            for j in range(4):
+                bank = psum.tile([P, HALF], F32, name="bank")
+                got.append(bank)
+            return got
+
+        def cols(half):
+            return slice(half * HALF, (half + 1) * HALF)
+
+        def exp1(half, banks):
+            for j in range(PACK):
+                nc.scalar.activation(out=lg[:, j, cols(half)], in_=banks[j][:], func=ACT.Exp)
+
+        def ln1(half, j):
+            nc.scalar.activation(
+                out=lg[:, j, cols(half)], in_=lg[:, j, cols(half)], func=ACT.Ln, bias=1.0
+            )
+
+        def softplus(half, banks, j):
+            nc.vector.scalar_tensor_tensor(
+                out=lg[:, j, cols(half)],
+                in0=lg[:, j, cols(half)],
+                scalar=20.0,
+                in1=banks[j][:],
+                op0=ALU.min,
+                op1=ALU.max,
+            )
+
+        def ln2(half, j):
+            nc.scalar.activation(
+                out=lg[:, j, cols(half)], in_=lg[:, j, cols(half)], func=ACT.Ln, bias=0.25
+            )
+
+        def exp2(a, b):
+            r = work.tile([P, P, PACK], F32, name="r", bufs=4)
+            nc.scalar.activation(
+                out=r[:], in_=lg[:, :, a:b].rearrange("p j c -> p c j"), func=ACT.Exp, scale=-1.0
+            )
+            return r
+
+        def ratio(a, b, r):
+            nc.vector.tensor_tensor(
+                out=e_int[:, a:b, :], in0=r[:], in1=v_int[:, a:b, :], op=ALU.mult
+            )
+
+        def gain2(a, width, u):
+            eg = work.tile([P, 256, PACK], BF16, name="eg", align_bytes=64)
+            nc.vector.scalar_tensor_tensor(
+                out=eg[:, 0:width, :],
+                in0=e_int[:, a + u : a + u + width, :],
+                scalar=-1.0,
+                in1=g2_t[:, u, :].unsqueeze(1).to_broadcast([P, width, PACK]),
+                op0=ALU.add,
+                op1=ALU.mult,
+            )
+            return eg
+
+        def mm2(banks, off, width, u, q):
+            for m in range(4):
+                nc.tensor.matmul_mx(
+                    out=banks[m][:, off : off + width],
+                    lhsT=w2w[:, u, m * P : (m + 1) * P].bitcast(FP8X4),
+                    lhsT_scale=w2s[4 * u : P, m * P : (m + 1) * P],
+                    rhs=q[0][:, 0:width].bitcast(FP8X4),
+                    rhs_scale=q[1][:, 0:width],
+                    start=(u == 0),
+                    stop=(u == TAPS - 1),
+                )
+
+        def stage2_unit(banks, a, width):
+            off = a % HALF
+            eg = {0: gain2(a, width, 0)}
+            for u in range(TAPS):
+                if u + 1 < TAPS:
+                    eg[u + 1] = gain2(a, width, u + 1)
+                mm2(banks, off, width, u, quant(eg[u], width, "eq"))
+
+        def finish(half, banks, m):
+            ex = work.tile([P, HALF], F32, name="ex")
+            nc.scalar.activation(
+                out=ex[:], in_=banks[m][:], func=ACT.Exp, scale=0.5, bias=mu_b[:, m : m + 1]
+            )
+            res = work.tile([P, HALF], F32, name="res")
+            nc.vector.tensor_tensor(out=res[:], in0=ex[:], in1=h_nat[:, m, cols(half)], op=ALU.mult)
+            nc.sync.dma_start(out=out_0[m * P : (m + 1) * P, cols(half)], in_=res[:])
+            resb = work.tile([P, HALF], BF16, name="resb", align_bytes=64)
+            nc.vector.tensor_copy(out=resb[:], in_=res[:])
+            return resb
+
+        def turn(bank, m, resb):
+            words = resb[:].bitcast(F32)
+            base = (m % 2) * 256
+            for x in range(2):
+                nc.tensor.transpose(
+                    bank[:, base + x * P : base + (x + 1) * P], words[:, x : 256 : 2], ident[:]
+                )
+
+        def planes(half, bank, pair):
+            pin = work.tile([P, 256, PACK], BF16, name="pin", align_bytes=64)
+            nc.scalar.copy(
+                out=pin[:].rearrange("p k b -> p (k b)").bitcast(F32).rearrange(
+                    "p (m k x) -> p m k x", m=2, x=2),
+                in_=bank[:].rearrange("p (m x k) -> p m k x", m=2, x=2),
+            )
+            return pin
+
+        lay(nc.vector.tensor_copy, h_int, 0, h_tail, 1, 4)
+        lay(nc.vector.tensor_copy, h_int, 3, h_raw, 0, 256)
+        lay(nc.scalar.copy, h_int, 3 + 256, h_raw, 256, 384)
+        lay(nc.scalar.copy, h_int, 3 + 384, h_raw, 384, 512)
+        for i in range(4):
+            lay(nc.scalar.copy, h_int, 3 + 512 + 128 * i, h_raw, 512 + 128 * i, 640 + 128 * i)
+        for i in range(4):
+            lay(nc.scalar.copy, v_int, 128 * i, v_raw, 128 * i, 128 * i + 128)
+
+        s_a = banks_of("a")
+        hg = {0: gain1(0, 0), 1: gain1(0, 1)}
+        q0 = quant(hg[0], HALF, "hq")
+        hg[2] = gain1(0, 2)
+        q1 = quant(hg[1], HALF, "hq")
+        permute_scales()
+        permute_words(0)
+        mm1(s_a, 0, q0)
+        permute_words(1)
+        mm1(s_a, 1, q1)
+        hg[3] = gain1(0, 3)
+        q = quant(hg[2], HALF, "hq")
+        permute_words(2)
+        mm1(s_a, 2, q)
+        permute_words(3)
+        q = quant(hg[3], HALF, "hq")
+        mm1(s_a, 3, q)
+
+        exp1(0, s_a)
+        for j in range(PACK):
+            ln1(0, j)
+
+        s_b = banks_of("b")
+        hg = {0: gain1(1, 0), 1: gain1(1, 1)}
+        mm1(s_b, 0, quant(hg[0], HALF, "hq"))
+        hg[2] = gain1(1, 2)
+        mm1(s_b, 1, quant(hg[1], HALF, "hq"))
+        softplus(0, s_a, 0)
+        softplus(0, s_a, 1)
+        ln2(0, 0)
+        ln2(0, 1)
+        hg[3] = gain1(1, 3)
+        softplus(0, s_a, 2)
+        softplus(0, s_a, 3)
+        ln2(0, 2)
+        ln2(0, 3)
+        mm1(s_b, 2, quant(hg[2], HALF, "hq"))
+        mm1(s_b, 3, quant(hg[3], HALF, "hq"))
+        lay(nc.vector.tensor_copy, v_int, 512, v_raw, 512, 768)
+        lay(nc.vector.tensor_copy, v_int, 768, v_raw, 768, 1024)
+        nc.vector.tensor_scalar(
+            out=mu_b[:], in0=mu_t[:, :, 0], scalar1=-0.5, scalar2=None, op0=ALU.mult
+        )
+        for i in range(4):
+            ratio(128 * i, 128 * i + 128, exp2(128 * i, 128 * i + 128))
+        nc.vector.tensor_copy(out=e_int[:, T : T + 3, :], in_=e_int[:, 0:3, :])
+
+        exp1(1, s_b)
+        for j in range(PACK):
+            ln1(1, j)
+
+        r_a = banks_of("a2")
+        stage2_unit(r_a, 0, 256)
+        for j in range(PACK):
+            softplus(1, s_b, j)
+            ln2(1, j)
+        stage2_unit(r_a, 256, 128)
+        for i in range(4):
+            ratio(512 + 128 * i, 640 + 128 * i, exp2(512 + 128 * i, 640 + 128 * i))
+        stage2_unit(r_a, 384, 128)
+
+        def tail(half, banks, fill=None):
+            pc = keep.tile([P, 512], U32, name="pc%d" % half, align_bytes=64)
+            ps = keep.tile([P, 512], U8, name="ps%d" % half, align_bytes=64)
+            exs = []
+            for m in range(4):
+                ex = work.tile([P, HALF], F32, name="ex", bufs=4)
+                nc.scalar.activation(
+                    out=ex[:], in_=banks[m][:], func=ACT.Exp, scale=0.5, bias=mu_b[:, m : m + 1]
+                )
+                exs.append(ex)
+            if fill:
+                fill()
+            res = []
+            resb = []
+            pins = []
+            tb = []
+
+            def mul(m):
+                o = work.tile([P, HALF], F32, name="res", bufs=4)
+                nc.vector.tensor_tensor(
+                    out=o[:], in0=exs[m][:], in1=h_nat[:, m, cols(half)], op=ALU.mult)
+                nc.sync.dma_start(out=out_0[m * P : (m + 1) * P, cols(half)], in_=o[:])
+                res.append(o)
+
+            def rnd(m):
+                o = work.tile([P, HALF], BF16, name="resb", align_bytes=64, bufs=4)
+                nc.vector.tensor_copy(out=o[:], in_=res[m][:])
+                resb.append(o)
+
+            def qp(pair):
+                nc.vector.quantize_mx(
+                    out=pc[:, 256 * pair : 256 * pair + 256].bitcast(FP8X4),
+                    scales=ps[:, 256 * pair : 256 * pair + 256],
+                    in_=pins[pair][:].rearrange("p k b -> p (k b)"),
+                )
+                nc.sync.dma_start(
+                    out=out_1[half].rearrange("p m b -> p (m b)").bitcast(I32)[
+                        :, 256 * pair : 256 * pair + 256],
+                    in_=pc[:, 256 * pair : 256 * pair + 256].bitcast(I32),
+                )
+
+            def trn(pair):
+                bank = psum.tile([P, HALF], F32, name="bank")
+                turn(bank, 2 * pair, resb[2 * pair])
+                turn(bank, 2 * pair + 1, resb[2 * pair + 1])
+                pins.append(planes(half, bank, pair))
+
+            mul(0)
+            mul(1)
+            rnd(0)
+            rnd(1)
+            trn(0)
+            mul(2)
+            mul(3)
+            rnd(2)
+            rnd(3)
+            trn(1)
+            qp(0)
+            qp(1)
+            for x in range(4):
+                nc.sync.dma_start(
+                    out=out_2[half, 4 * x : 4 * x + 4, :].bitcast(I32),
+                    in_=ps[32 * x : 32 * x + 4, :].bitcast(I32),
+                )
+
+        r_b = banks_of("b2")
+        stage2_unit(r_b, 512, 256)
+        tail(0, r_a)
+        stage2_unit(r_b, 768, 256)
+        tail(1, r_b)

@@ -18,7 +18,6 @@ PACK = 4
 T = 1024
 HALF = 512
 FLOPS = 2 * 2 * 512 * 2048 * 1024
-EXP_QUARTER = 1.2840254166877414
 
 
 def tile_convolutivenmfexponentiatedupdate_x2_kernel(
@@ -28,7 +27,7 @@ def tile_convolutivenmfexponentiatedupdate_x2_kernel(
     with ExitStack() as ctx:
         keep = ctx.enter_context(tc.tile_pool(name="keep", bufs=1))
         work = ctx.enter_context(tc.tile_pool(name="work", bufs=3))
-        psum = ctx.enter_context(tc.psum_pool(name="psum", bufs=8))
+        psum = ctx.enter_context(tc.psum_pool(name="psum", bufs=4))
         ctx.enter_context(tc.manual_schedule())
 
         warm = keep.tile([P, 1], F32, name="warm")
@@ -36,7 +35,6 @@ def tile_convolutivenmfexponentiatedupdate_x2_kernel(
         g2_t = keep.tile([P, TAPS, PACK], BF16, name="g2_t")
         mu_t = keep.tile([P, 4, 2], BF16, name="mu_t")
         mu_b = keep.tile([P, 4], F32, name="mu_b")
-        h_tail = keep.tile([P, PACK, 4], BF16, name="h_tail")
         h_raw = keep.tile([P, PACK, T], BF16, name="h_raw")
         h_int = keep.tile([P, 3 + T, PACK], BF16, name="h_int")
         h_nat = keep.tile([P, 4, T], BF16, name="h_nat")
@@ -52,18 +50,17 @@ def tile_convolutivenmfexponentiatedupdate_x2_kernel(
         lg = keep.tile([P, PACK, T], F32, name="lg")
         e_int = keep.tile([P, T + 3, PACK], F32, name="e_int")
 
-        nc.vector.memset(warm[:], 0.0)
-        nc.scalar.activation(out=warm[:], in_=warm[:], func=ACT.Exp)
-        nc.vector.memset(w1s_raw[:].bitcast(I32), 0)
-        nc.gpsimd.memset(w2s[:].bitcast(I32), 0)
-        make_identity(nc, ident[:])
-
         h_pj = h.rearrange("(p j) t -> p j t", j=PACK)
         v_pj = v.rearrange("(p j) t -> p j t", j=PACK)
-        nc.sync.dma_start(out=g1_t[:], in_=g1.rearrange("(u p j) -> p u j", u=TAPS, j=PACK))
-        nc.sync.dma_start(out=h_tail[:], in_=h_pj[:, :, T - 4 : T])
-        nc.sync.dma_start(out=h_raw[:, :, 0:HALF], in_=h_pj[:, :, 0:HALF])
+        nc.scalar.dma_start(out=g1_t[:], in_=g1.rearrange("(u p j) -> p u j", u=TAPS, j=PACK))
+        nc.sync.dma_start(out=h_raw[:, :, 240:512], in_=h_pj[:, :, 240:512])
+        nc.sync.dma_start(out=h_raw[:, :, 0:240], in_=h_pj[:, :, 0:240])
         nc.sync.dma_start(out=h_raw[:, :, HALF:T], in_=h_pj[:, :, HALF:T])
+        nc.vector.memset(warm[:], 0.0)
+        nc.vector.memset(w1s_raw[:].bitcast(I32), 0)
+        nc.vector.memset(w2s[:].bitcast(I32), 0)
+        nc.scalar.activation(out=warm[:], in_=warm[:], func=ACT.Exp)
+        make_identity(nc, ident[:])
         nc.sync.dma_start(out=v_raw[:, :, 0:HALF], in_=v_pj[:, :, 0:HALF])
         for q in range(4):
             nc.sync.dma_start(
@@ -74,11 +71,11 @@ def tile_convolutivenmfexponentiatedupdate_x2_kernel(
             nc.sync.dma_start(
                 out=w1w_raw[:, u, :], in_=w1_words[u].rearrange("p n b -> p (n b)").bitcast(I32)
             )
+        nc.sync.dma_start(out=v_raw[:, :, HALF:T], in_=v_pj[:, :, HALF:T])
         nc.gpsimd.dma_start(out=g2_t[:], in_=g2.rearrange("(u p j) -> p u j", u=TAPS, j=PACK))
         nc.gpsimd.dma_start(
             out=mu_t[:, :, 0:1], in_=mu.rearrange("(m p o) -> p m o", m=4, o=1)
         )
-        nc.sync.dma_start(out=v_raw[:, :, HALF:T], in_=v_pj[:, :, HALF:T])
         for q in range(4):
             nc.sync.dma_start(
                 out=w2s[32 * q : 32 * q + 16, :].bitcast(I32),
@@ -95,20 +92,20 @@ def tile_convolutivenmfexponentiatedupdate_x2_kernel(
                 out=dst[:, dst0 : dst0 + b - a, :], in_=src[:, :, a:b].rearrange("p j c -> p c j")
             )
 
-        def gain1(half, u):
-            hg = work.tile([P, HALF, PACK], BF16, name="hg", align_bytes=64)
-            c0 = half * HALF + 3 - u
+        def gain1(c0, width, u):
+            hg = work.tile([P, HALF, PACK], BF16, name="hg", align_bytes=64, bufs=3)
+            a = c0 + 3 - u
             nc.vector.tensor_tensor(
-                out=hg[:],
-                in0=h_int[:, c0 : c0 + HALF, :],
-                in1=g1_t[:, u, :].unsqueeze(1).to_broadcast([P, HALF, PACK]),
+                out=hg[:, 0:width, :],
+                in0=h_int[:, a : a + width, :],
+                in1=g1_t[:, u, :].unsqueeze(1).to_broadcast([P, width, PACK]),
                 op=ALU.mult,
             )
             return hg
 
-        def quant(src, width, name):
-            codes = work.tile([P, HALF], U32, name=name + "_c", align_bytes=64, bufs=6)
-            scales = work.tile([P, HALF], U8, name=name + "_s", align_bytes=64, bufs=6)
+        def quant(src, width, name, cols, bufs):
+            codes = work.tile([P, cols], U32, name=name + "_c", align_bytes=64, bufs=bufs)
+            scales = work.tile([P, cols], U8, name=name + "_s", align_bytes=64, bufs=bufs)
             nc.vector.quantize_mx(
                 out=codes[:, 0:width].bitcast(FP8X4),
                 scales=scales[:, 0:width],
@@ -116,14 +113,14 @@ def tile_convolutivenmfexponentiatedupdate_x2_kernel(
             )
             return codes, scales
 
-        def mm1(banks, u, q):
+        def mm1(banks, off, width, u, q):
             for j in range(PACK):
                 nc.tensor.matmul_mx(
-                    out=banks[j][:],
+                    out=banks[j][:, off : off + width],
                     lhsT=w1w[:, u, j, :].bitcast(FP8X4),
                     lhsT_scale=w1s[4 * u : P, j, :],
-                    rhs=q[0][:].bitcast(FP8X4),
-                    rhs_scale=q[1][:],
+                    rhs=q[0][:, 0:width].bitcast(FP8X4),
+                    rhs_scale=q[1][:, 0:width],
                     start=(u == 0),
                     stop=(u == TAPS - 1),
                 )
@@ -139,19 +136,18 @@ def tile_convolutivenmfexponentiatedupdate_x2_kernel(
                 in_=w1s_raw[:].rearrange("p (m j) -> p m j", j=PACK),
             )
 
+        def bank_of(tag):
+            bank = psum.tile([P, HALF], F32, name=tag, bufs=4)
+            return bank
+
         def banks_of(tag):
-            got = []
-            for j in range(4):
-                bank = psum.tile([P, HALF], F32, name="bank")
-                got.append(bank)
-            return got
+            return [bank_of(tag) for j in range(4)]
 
         def cols(half):
             return slice(half * HALF, (half + 1) * HALF)
 
-        def exp1(half, banks):
-            for j in range(PACK):
-                nc.scalar.activation(out=lg[:, j, cols(half)], in_=banks[j][:], func=ACT.Exp)
+        def exp1(half, banks, j):
+            nc.scalar.activation(out=lg[:, j, cols(half)], in_=banks[j][:], func=ACT.Exp)
 
         def ln1(half, j):
             nc.scalar.activation(
@@ -173,20 +169,26 @@ def tile_convolutivenmfexponentiatedupdate_x2_kernel(
                 out=lg[:, j, cols(half)], in_=lg[:, j, cols(half)], func=ACT.Ln, bias=0.25
             )
 
-        def exp2(a, b):
+        def exp2(i):
             r = work.tile([P, P, PACK], F32, name="r", bufs=4)
             nc.scalar.activation(
-                out=r[:], in_=lg[:, :, a:b].rearrange("p j c -> p c j"), func=ACT.Exp, scale=-1.0
+                out=r[:],
+                in_=lg[:, :, i * P : (i + 1) * P].rearrange("p j c -> p c j"),
+                func=ACT.Exp,
+                scale=-1.0,
             )
             return r
 
-        def ratio(a, b, r):
+        def ratio(i, r):
             nc.vector.tensor_tensor(
-                out=e_int[:, a:b, :], in0=r[:], in1=v_int[:, a:b, :], op=ALU.mult
+                out=e_int[:, i * P : (i + 1) * P, :],
+                in0=r[:],
+                in1=v_int[:, i * P : (i + 1) * P, :],
+                op=ALU.mult,
             )
 
         def gain2(a, width, u):
-            eg = work.tile([P, 256, PACK], BF16, name="eg", align_bytes=64)
+            eg = work.tile([P, 256, PACK], BF16, name="eg", align_bytes=64, bufs=6)
             nc.vector.scalar_tensor_tensor(
                 out=eg[:, 0:width, :],
                 in0=e_int[:, a + u : a + u + width, :],
@@ -209,180 +211,261 @@ def tile_convolutivenmfexponentiatedupdate_x2_kernel(
                     stop=(u == TAPS - 1),
                 )
 
-        def stage2_unit(banks, a, width):
+        def stage1_unit(banks, c0, width, between, first={}):
+            off = c0 % HALF
+            hg = {0: gain1(c0, width, 0)}
+            for u in range(TAPS):
+                if u + 1 < TAPS:
+                    hg[u + 1] = gain1(c0, width, u + 1)
+                for f in between.get(u, []):
+                    f()
+                if width == HALF:
+                    q = quant(hg[u], width, "hq", HALF, 4)
+                else:
+                    q = quant(hg[u], width, "hqa", 256, 8)
+                for f in first.get(u, []):
+                    f()
+                mm1(banks, off, width, u, q)
+
+        def stage2_unit(banks, a, width, between):
             off = a % HALF
             eg = {0: gain2(a, width, 0)}
             for u in range(TAPS):
                 if u + 1 < TAPS:
                     eg[u + 1] = gain2(a, width, u + 1)
-                mm2(banks, off, width, u, quant(eg[u], width, "eq"))
+                for f in between.get(u, []):
+                    f()
+                mm2(banks, off, width, u, quant(eg[u], width, "eq", 256, 8))
 
-        def finish(half, banks, m):
-            ex = work.tile([P, HALF], F32, name="ex")
+        fin = {}
+        for half in range(2):
+            for m in range(4):
+                rb = keep.tile([P, HALF], BF16, name="rb%d%d" % (half, m), align_bytes=64)
+                fin[half, m] = rb
+        pcs = []
+        for half in range(2):
+            pc = keep.tile([P, 512], U32, name="pc%d" % half, align_bytes=64)
+            ps = keep.tile([P, 512], U8, name="ps%d" % half, align_bytes=64)
+            pcs.append((pc, ps))
+
+        def fexp(banks, m, a, width):
+            ex = work.tile([P, HALF], F32, name="ex", bufs=6)
             nc.scalar.activation(
-                out=ex[:], in_=banks[m][:], func=ACT.Exp, scale=0.5, bias=mu_b[:, m : m + 1]
+                out=ex[:, 0:width],
+                in_=banks[m][:, a % HALF : a % HALF + width],
+                func=ACT.Exp,
+                scale=0.5,
+                bias=mu_b[:, m : m + 1],
             )
-            res = work.tile([P, HALF], F32, name="res")
-            nc.vector.tensor_tensor(out=res[:], in0=ex[:], in1=h_nat[:, m, cols(half)], op=ALU.mult)
-            nc.sync.dma_start(out=out_0[m * P : (m + 1) * P, cols(half)], in_=res[:])
-            resb = work.tile([P, HALF], BF16, name="resb", align_bytes=64)
-            nc.vector.tensor_copy(out=resb[:], in_=res[:])
-            return resb
+            return ex
 
-        def turn(bank, m, resb):
-            words = resb[:].bitcast(F32)
-            base = (m % 2) * 256
-            for x in range(2):
-                nc.tensor.transpose(
-                    bank[:, base + x * P : base + (x + 1) * P], words[:, x : 256 : 2], ident[:]
-                )
+        def fmul(ex, m, a, width):
+            res = work.tile([P, HALF], F32, name="res", bufs=8)
+            nc.vector.tensor_tensor(
+                out=res[:, 0:width], in0=ex[:, 0:width], in1=h_nat[:, m, a : a + width], op=ALU.mult
+            )
+            nc.sync.dma_start(out=out_0[m * P : (m + 1) * P, a : a + width], in_=res[:, 0:width])
+            return res
 
-        def planes(half, bank, pair):
+        def fround(engine_copy, res, m, a, width):
+            engine_copy(
+                out=fin[a // HALF, m][:, a % HALF : a % HALF + width], in_=res[:, 0:width]
+            )
+
+        def turn(half, pair):
+            bank = bank_of("by")
+            for k in range(2):
+                words = fin[half, 2 * pair + k][:].bitcast(F32)
+                for x in range(2):
+                    base = k * 256 + x * P
+                    nc.tensor.transpose(bank[:, base : base + P], words[:, x:256:2], ident[:])
+            return bank
+
+        def pinlay(engine_copy, bank):
             pin = work.tile([P, 256, PACK], BF16, name="pin", align_bytes=64)
-            nc.scalar.copy(
+            engine_copy(
                 out=pin[:].rearrange("p k b -> p (k b)").bitcast(F32).rearrange(
                     "p (m k x) -> p m k x", m=2, x=2),
                 in_=bank[:].rearrange("p (m x k) -> p m k x", m=2, x=2),
             )
             return pin
 
-        lay(nc.vector.tensor_copy, h_int, 0, h_tail, 1, 4)
-        lay(nc.vector.tensor_copy, h_int, 3, h_raw, 0, 256)
-        lay(nc.scalar.copy, h_int, 3 + 256, h_raw, 256, 384)
-        lay(nc.scalar.copy, h_int, 3 + 384, h_raw, 384, 512)
-        for i in range(4):
-            lay(nc.scalar.copy, h_int, 3 + 512 + 128 * i, h_raw, 512 + 128 * i, 640 + 128 * i)
-        for i in range(4):
-            lay(nc.scalar.copy, v_int, 128 * i, v_raw, 128 * i, 128 * i + 128)
+        def planes(half, pair, pin):
+            pc, ps = pcs[half]
+            at = slice(256 * pair, 256 * pair + 256)
+            nc.vector.quantize_mx(
+                out=pc[:, at].bitcast(FP8X4),
+                scales=ps[:, at],
+                in_=pin[:].rearrange("p k b -> p (k b)"),
+            )
+            nc.sync.dma_start(
+                out=out_1[half].rearrange("p m b -> p (m b)").bitcast(I32)[:, at],
+                in_=pc[:, at].bitcast(I32),
+            )
 
-        s_a = banks_of("a")
-        hg = {0: gain1(0, 0), 1: gain1(0, 1)}
-        q0 = quant(hg[0], HALF, "hq")
-        hg[2] = gain1(0, 2)
-        q1 = quant(hg[1], HALF, "hq")
-        permute_scales()
-        permute_words(0)
-        mm1(s_a, 0, q0)
-        permute_words(1)
-        mm1(s_a, 1, q1)
-        hg[3] = gain1(0, 3)
-        q = quant(hg[2], HALF, "hq")
-        permute_words(2)
-        mm1(s_a, 2, q)
-        permute_words(3)
-        q = quant(hg[3], HALF, "hq")
-        mm1(s_a, 3, q)
-
-        exp1(0, s_a)
-        for j in range(PACK):
-            ln1(0, j)
-
-        s_b = banks_of("b")
-        hg = {0: gain1(1, 0), 1: gain1(1, 1)}
-        mm1(s_b, 0, quant(hg[0], HALF, "hq"))
-        hg[2] = gain1(1, 2)
-        mm1(s_b, 1, quant(hg[1], HALF, "hq"))
-        softplus(0, s_a, 0)
-        softplus(0, s_a, 1)
-        ln2(0, 0)
-        ln2(0, 1)
-        hg[3] = gain1(1, 3)
-        softplus(0, s_a, 2)
-        softplus(0, s_a, 3)
-        ln2(0, 2)
-        ln2(0, 3)
-        mm1(s_b, 2, quant(hg[2], HALF, "hq"))
-        mm1(s_b, 3, quant(hg[3], HALF, "hq"))
-        lay(nc.vector.tensor_copy, v_int, 512, v_raw, 512, 768)
-        lay(nc.vector.tensor_copy, v_int, 768, v_raw, 768, 1024)
-        nc.vector.tensor_scalar(
-            out=mu_b[:], in0=mu_t[:, :, 0], scalar1=-0.5, scalar2=None, op0=ALU.mult
-        )
-        for i in range(4):
-            ratio(128 * i, 128 * i + 128, exp2(128 * i, 128 * i + 128))
-        nc.vector.tensor_copy(out=e_int[:, T : T + 3, :], in_=e_int[:, 0:3, :])
-
-        exp1(1, s_b)
-        for j in range(PACK):
-            ln1(1, j)
-
-        r_a = banks_of("a2")
-        stage2_unit(r_a, 0, 256)
-        for j in range(PACK):
-            softplus(1, s_b, j)
-            ln2(1, j)
-        stage2_unit(r_a, 256, 128)
-        for i in range(4):
-            ratio(512 + 128 * i, 640 + 128 * i, exp2(512 + 128 * i, 640 + 128 * i))
-        stage2_unit(r_a, 384, 128)
-
-        def tail(half, banks, fill=None):
-            pc = keep.tile([P, 512], U32, name="pc%d" % half, align_bytes=64)
-            ps = keep.tile([P, 512], U8, name="ps%d" % half, align_bytes=64)
-            exs = []
-            for m in range(4):
-                ex = work.tile([P, HALF], F32, name="ex", bufs=4)
-                nc.scalar.activation(
-                    out=ex[:], in_=banks[m][:], func=ACT.Exp, scale=0.5, bias=mu_b[:, m : m + 1]
-                )
-                exs.append(ex)
-            if fill:
-                fill()
-            res = []
-            resb = []
-            pins = []
-            tb = []
-
-            def mul(m):
-                o = work.tile([P, HALF], F32, name="res", bufs=4)
-                nc.vector.tensor_tensor(
-                    out=o[:], in0=exs[m][:], in1=h_nat[:, m, cols(half)], op=ALU.mult)
-                nc.sync.dma_start(out=out_0[m * P : (m + 1) * P, cols(half)], in_=o[:])
-                res.append(o)
-
-            def rnd(m):
-                o = work.tile([P, HALF], BF16, name="resb", align_bytes=64, bufs=4)
-                nc.vector.tensor_copy(out=o[:], in_=res[m][:])
-                resb.append(o)
-
-            def qp(pair):
-                nc.vector.quantize_mx(
-                    out=pc[:, 256 * pair : 256 * pair + 256].bitcast(FP8X4),
-                    scales=ps[:, 256 * pair : 256 * pair + 256],
-                    in_=pins[pair][:].rearrange("p k b -> p (k b)"),
-                )
-                nc.sync.dma_start(
-                    out=out_1[half].rearrange("p m b -> p (m b)").bitcast(I32)[
-                        :, 256 * pair : 256 * pair + 256],
-                    in_=pc[:, 256 * pair : 256 * pair + 256].bitcast(I32),
-                )
-
-            def trn(pair):
-                bank = psum.tile([P, HALF], F32, name="bank")
-                turn(bank, 2 * pair, resb[2 * pair])
-                turn(bank, 2 * pair + 1, resb[2 * pair + 1])
-                pins.append(planes(half, bank, pair))
-
-            mul(0)
-            mul(1)
-            rnd(0)
-            rnd(1)
-            trn(0)
-            mul(2)
-            mul(3)
-            rnd(2)
-            rnd(3)
-            trn(1)
-            qp(0)
-            qp(1)
+        def scales_out(half):
             for x in range(4):
                 nc.sync.dma_start(
                     out=out_2[half, 4 * x : 4 * x + 4, :].bitcast(I32),
-                    in_=ps[32 * x : 32 * x + 4, :].bitcast(I32),
+                    in_=pcs[half][1][32 * x : 32 * x + 4, :].bitcast(I32),
                 )
 
-        r_b = banks_of("b2")
-        stage2_unit(r_b, 512, 256)
-        tail(0, r_a)
-        stage2_unit(r_b, 768, 256)
-        tail(1, r_b)
+        diag = keep.tile([P, 3, PACK, P], F32, name="diag")
+        for u in range(1, TAPS):
+            for j in range(PACK):
+                nc.gpsimd.tensor_scalar(
+                    out=diag[:, u - 1, j, :], in0=ident[:], scalar1=g2_t[:, u, j : j + 1],
+                    scalar2=0.0, op0=ALU.mult, op1=ALU.add)
+
+        vcopy = nc.vector.tensor_copy
+        scopy = nc.scalar.copy
+        lay(vcopy, h_int, 3 + 240, h_raw, 240, 416)
+        lay(scopy, h_int, 3 + 416, h_raw, 416, 512)
+        lay(scopy, h_int, 3, h_raw, 0, 128)
+        lay(scopy, h_int, 3 + 128, h_raw, 128, 240)
+        lay(scopy, h_int, 0, h_raw, T - 3, T)
+        for i in range(4):
+            lay(scopy, h_int, 515 + 128 * i, h_raw, 512 + 128 * i, 640 + 128 * i)
+        for i in range(8):
+            lay(scopy, v_int, 128 * i, v_raw, 128 * i, 128 * i + 128)
+
+        s_a = banks_of("bx")
+        qs = []
+        hg = [gain1(256, 256, 0), gain1(256, 256, 1)]
+        for u in range(TAPS):
+            qs.append(quant(hg[u], 256, "hqa", 256, 8))
+            if u + 2 < TAPS:
+                hg.append(gain1(256, 256, u + 2))
+        h2 = [gain1(0, 256, 0), gain1(0, 256, 1)]
+        permute_scales()
+        permute_words(0)
+        mm1(s_a, 256, 256, 0, qs[0])
+        permute_words(1)
+        mm1(s_a, 256, 256, 1, qs[1])
+        permute_words(2)
+        mm1(s_a, 256, 256, 2, qs[2])
+        permute_words(3)
+        mm1(s_a, 256, 256, 3, qs[3])
+        for u in range(TAPS):
+            q = quant(h2[u], 256, "hqa", 256, 8)
+            if u + 2 < TAPS:
+                h2.append(gain1(0, 256, u + 2))
+            mm1(s_a, 0, 256, u, q)
+
+        for j in range(PACK):
+            exp1(0, s_a, j)
+        for j in range(PACK):
+            ln1(0, j)
+
+        s_b = banks_of("by")
+
+        def soft_a(j):
+            softplus(0, s_a, j)
+            ln2(0, j)
+
+        def soft_b(j):
+            softplus(1, s_b, j)
+            ln2(1, j)
+
+        stage1_unit(
+            s_b, 512, 512,
+            {2: [lambda: soft_a(0), lambda: soft_a(1)], 3: [lambda: soft_a(2), lambda: soft_a(3)]},
+        )
+        nc.vector.tensor_scalar(
+            out=mu_b[:], in0=mu_t[:, :, 0], scalar1=-0.5, scalar2=None, op0=ALU.mult
+        )
+        rs = [exp2(i) for i in range(4)]
+        for j in range(PACK):
+            exp1(1, s_b, j)
+        for j in range(PACK):
+            ln1(1, j)
+
+        r_a = banks_of("bx")
+        ratio(0, rs[0])
+        vcopy(out=e_int[:, T : T + 3, :], in_=e_int[:, 0:3, :])
+        ratio(1, rs[1])
+        stage2_unit(r_a, 0, 128, {})
+        ratio(2, rs[2])
+        ratio(3, rs[3])
+        stage2_unit(
+            r_a, 128, 256,
+            {0: [lambda: soft_b(0), lambda: soft_b(1), lambda: soft_b(2), lambda: soft_b(3)]},
+        )
+        rs = [exp2(i) for i in range(4, 8)]
+        r_b = banks_of("bx")
+        for i in range(4):
+            ratio(4 + i, rs[i])
+        em1 = keep.tile([P, 260, PACK], F32, name="em1")
+        for a, b in ((0, 131), (131, 260)):
+            nc.scalar.activation(
+                out=em1[:, a:b, :], in_=e_int[:, 640 + a : 640 + b, :], func=ACT.Identity, bias=-1.0
+            )
+        pe_eg = {}
+
+        def gain2_pe(u):
+            eg = work.tile([P, 256, PACK], BF16, name="egp", align_bytes=64, bufs=4)
+            for i in range(2):
+                bank = bank_of("by")
+                for j in range(PACK):
+                    nc.tensor.matmul(
+                        out=bank[:, j * P : (j + 1) * P],
+                        lhsT=diag[:, u - 1, j, :],
+                        rhs=em1[:, i * P + u : (i + 1) * P + u, j],
+                        start=True,
+                        stop=True,
+                    )
+                nc.scalar.copy(
+                    out=eg[:, i * P : (i + 1) * P, :],
+                    in_=bank[:].rearrange("p (j c) -> p c j", j=PACK),
+                )
+            pe_eg[u] = eg
+
+        ex_a = {}
+
+        def out_a(m, eng):
+            fround(eng, fmul(ex_a[m], m, 0, HALF), m, 0, HALF)
+
+        def mmq(banks, off, width, u, eg):
+            mm2(banks, off, width, u, quant(eg, width, "eq", 256, 8))
+
+        eg = [gain2(384, 128, u) for u in range(TAPS)]
+        gain2_pe(1)
+        for u in range(TAPS):
+            mmq(r_a, 384, 128, u, eg[u])
+        for m in range(4):
+            ex_a[m] = fexp(r_a, m, 0, HALF)
+        gain2_pe(2)
+        eg = [gain2(512, 128, u) for u in range(TAPS)]
+        for u in range(TAPS):
+            mmq(r_b, 0, 128, u, eg[u])
+        gain2_pe(3)
+        out_a(0, scopy)
+        mmq(r_b, 128, 256, 0, gain2(640, 256, 0))
+        out_a(1, scopy)
+        mmq(r_b, 128, 256, 1, pe_eg[1])
+
+        out_a(2, scopy)
+        out_a(3, scopy)
+        mmq(r_b, 128, 256, 2, pe_eg[2])
+        e7 = [gain2(896, 128, u) for u in range(TAPS)]
+        mmq(r_b, 128, 256, 3, pe_eg[3])
+        ex_b = [fexp(r_b, m, 512, 384) for m in range(4)]
+        for u in range(TAPS):
+            mmq(r_b, 384, 128, u, e7[u])
+        pin_a = [pinlay(scopy, turn(0, k)) for k in range(2)]
+        res = [fmul(ex_b[m], m, 512, 384) for m in range(4)]
+        ex_c = [fexp(r_b, m, 896, 128) for m in range(4)]
+        for m in range(4):
+            fround(scopy if m % 2 else vcopy, res[m], m, 512, 384)
+        planes(0, 0, pin_a[0])
+        planes(0, 1, pin_a[1])
+        scales_out(0)
+        p = [None, None]
+        for k in range(2):
+            res = [fmul(ex_c[m], m, 896, 128) for m in (2 * k, 2 * k + 1)]
+            for i in range(2):
+                fround(vcopy, res[i], 2 * k + i, 896, 128)
+            p[k] = pinlay(scopy if k == 0 else vcopy, turn(1, k))
+        planes(1, 0, p[0])
+        planes(1, 1, p[1])
+        scales_out(1)

@@ -36,7 +36,7 @@ def tile_convolutivenmfexponentiatedupdate_x2_kernel(
         mu_t = keep.tile([P, 4, 2], BF16, name="mu_t")
         mu_b = keep.tile([P, 4], F32, name="mu_b")
         h_raw = keep.tile([P, PACK, T], BF16, name="h_raw")
-        h_int = keep.tile([P, 3 + T, PACK], BF16, name="h_int")
+        h_int = keep.tile([P, 3 + HALF, PACK], BF16, name="h_int")
         h_nat = keep.tile([P, 4, T], BF16, name="h_nat")
         v_raw = keep.tile([P, PACK, T], BF16, name="v_raw")
         v_int = keep.tile([P, T, PACK], BF16, name="v_int")
@@ -47,21 +47,24 @@ def tile_convolutivenmfexponentiatedupdate_x2_kernel(
         w2w = keep.tile([P, TAPS, 512], I32, name="w2w", align_bytes=64)
         w2s = keep.tile([P, 512], U8, name="w2s", align_bytes=64)
         ident = keep.tile([P, P], F32, name="ident")
+        ident_b = keep.tile([P, P], BF16, name="ident_b")
+        diag = keep.tile([P, TAPS, PACK, P], BF16, name="diag")
+        g2f = keep.tile([P, TAPS, PACK], F32, name="g2f")
+        ng2f = keep.tile([P, TAPS, PACK], F32, name="ng2f")
         lg = keep.tile([P, PACK, T], F32, name="lg")
         e_int = keep.tile([P, T + 3, PACK], F32, name="e_int")
 
         h_pj = h.rearrange("(p j) t -> p j t", j=PACK)
         v_pj = v.rearrange("(p j) t -> p j t", j=PACK)
         nc.scalar.dma_start(out=g1_t[:], in_=g1.rearrange("(u p j) -> p u j", u=TAPS, j=PACK))
-        nc.sync.dma_start(out=h_raw[:, :, 240:512], in_=h_pj[:, :, 240:512])
-        nc.sync.dma_start(out=h_raw[:, :, 0:240], in_=h_pj[:, :, 0:240])
-        nc.sync.dma_start(out=h_raw[:, :, HALF:T], in_=h_pj[:, :, HALF:T])
+        for a, b in ((752, T), (496, 752), (0, 496)):
+            nc.sync.dma_start(out=h_raw[:, :, a:b], in_=h_pj[:, :, a:b])
         nc.vector.memset(warm[:], 0.0)
         nc.vector.memset(w1s_raw[:].bitcast(I32), 0)
         nc.vector.memset(w2s[:].bitcast(I32), 0)
         nc.scalar.activation(out=warm[:], in_=warm[:], func=ACT.Exp)
+        make_identity(nc, ident_b[:])
         make_identity(nc, ident[:])
-        nc.sync.dma_start(out=v_raw[:, :, 0:HALF], in_=v_pj[:, :, 0:HALF])
         for q in range(4):
             nc.sync.dma_start(
                 out=w1s_raw[32 * q : 32 * q + 16, :].bitcast(I32),
@@ -71,7 +74,8 @@ def tile_convolutivenmfexponentiatedupdate_x2_kernel(
             nc.sync.dma_start(
                 out=w1w_raw[:, u, :], in_=w1_words[u].rearrange("p n b -> p (n b)").bitcast(I32)
             )
-        nc.sync.dma_start(out=v_raw[:, :, HALF:T], in_=v_pj[:, :, HALF:T])
+        for a in (HALF, 0):
+            nc.sync.dma_start(out=v_raw[:, :, a : a + HALF], in_=v_pj[:, :, a : a + HALF])
         nc.gpsimd.dma_start(out=g2_t[:], in_=g2.rearrange("(u p j) -> p u j", u=TAPS, j=PACK))
         nc.gpsimd.dma_start(
             out=mu_t[:, :, 0:1], in_=mu.rearrange("(m p o) -> p m o", m=4, o=1)
@@ -92,13 +96,13 @@ def tile_convolutivenmfexponentiatedupdate_x2_kernel(
                 out=dst[:, dst0 : dst0 + b - a, :], in_=src[:, :, a:b].rearrange("p j c -> p c j")
             )
 
-        def gain1(c0, width, u):
+        def gain1(u):
             hg = work.tile([P, HALF, PACK], BF16, name="hg", align_bytes=64, bufs=3)
-            a = c0 + 3 - u
+            a = 3 - u
             nc.vector.tensor_tensor(
-                out=hg[:, 0:width, :],
-                in0=h_int[:, a : a + width, :],
-                in1=g1_t[:, u, :].unsqueeze(1).to_broadcast([P, width, PACK]),
+                out=hg[:],
+                in0=h_int[:, a : a + HALF, :],
+                in1=g1_t[:, u, :].unsqueeze(1).to_broadcast([P, HALF, PACK]),
                 op=ALU.mult,
             )
             return hg
@@ -113,7 +117,7 @@ def tile_convolutivenmfexponentiatedupdate_x2_kernel(
             )
             return codes, scales
 
-        def mm1(banks, off, width, u, q):
+        def mm1(banks, off, width, u, q, first, last):
             for j in range(PACK):
                 nc.tensor.matmul_mx(
                     out=banks[j][:, off : off + width],
@@ -121,8 +125,8 @@ def tile_convolutivenmfexponentiatedupdate_x2_kernel(
                     lhsT_scale=w1s[4 * u : P, j, :],
                     rhs=q[0][:, 0:width].bitcast(FP8X4),
                     rhs_scale=q[1][:, 0:width],
-                    start=(u == 0),
-                    stop=(u == TAPS - 1),
+                    start=first,
+                    stop=last,
                 )
 
         def permute_words(u):
@@ -132,8 +136,7 @@ def tile_convolutivenmfexponentiatedupdate_x2_kernel(
 
         def permute_scales():
             nc.vector.tensor_copy(
-                out=w1s[:].rearrange("p j m -> p m j"),
-                in_=w1s_raw[:].rearrange("p (m j) -> p m j", j=PACK),
+                out=w1s[:], in_=w1s_raw[:].rearrange("p (m j) -> p j m", j=PACK)
             )
 
         def bank_of(tag):
@@ -199,7 +202,9 @@ def tile_convolutivenmfexponentiatedupdate_x2_kernel(
             )
             return eg
 
-        def mm2(banks, off, width, u, q):
+        def mm2(banks, off, width, u, q, first=None, last=None):
+            first = u == 0 if first is None else first
+            last = u == TAPS - 1 if last is None else last
             for m in range(4):
                 nc.tensor.matmul_mx(
                     out=banks[m][:, off : off + width],
@@ -207,25 +212,9 @@ def tile_convolutivenmfexponentiatedupdate_x2_kernel(
                     lhsT_scale=w2s[4 * u : P, m * P : (m + 1) * P],
                     rhs=q[0][:, 0:width].bitcast(FP8X4),
                     rhs_scale=q[1][:, 0:width],
-                    start=(u == 0),
-                    stop=(u == TAPS - 1),
+                    start=first,
+                    stop=last,
                 )
-
-        def stage1_unit(banks, c0, width, between, first={}):
-            off = c0 % HALF
-            hg = {0: gain1(c0, width, 0)}
-            for u in range(TAPS):
-                if u + 1 < TAPS:
-                    hg[u + 1] = gain1(c0, width, u + 1)
-                for f in between.get(u, []):
-                    f()
-                if width == HALF:
-                    q = quant(hg[u], width, "hq", HALF, 4)
-                else:
-                    q = quant(hg[u], width, "hqa", 256, 8)
-                for f in first.get(u, []):
-                    f()
-                mm1(banks, off, width, u, q)
 
         def stage2_unit(banks, a, width, between):
             off = a % HALF
@@ -236,6 +225,44 @@ def tile_convolutivenmfexponentiatedupdate_x2_kernel(
                 for f in between.get(u, []):
                     f()
                 mm2(banks, off, width, u, quant(eg[u], width, "eq", 256, 8))
+
+        def gain2_s(a, width, u):
+            eg = work.tile([P, 256, PACK], BF16, name="egs", align_bytes=64, bufs=3)
+            for j in range(PACK):
+                nc.scalar.activation(
+                    out=eg[:, 0:width, j],
+                    in_=e_int[:, a + u : a + u + width, j],
+                    func=ACT.Identity,
+                    scale=g2f[:, u, j : j + 1],
+                    bias=ng2f[:, u, j : j + 1],
+                )
+            return eg
+
+        def gain1_v(c0, u):
+            hs = work.tile([P, 256, PACK], BF16, name="hs", bufs=1)
+            lay(nc.vector.tensor_copy, hs, 0, h_raw, c0 - u, c0 - u + 256)
+            hg = work.tile([P, 256, PACK], BF16, name="hgv", align_bytes=64, bufs=1)
+            nc.vector.tensor_tensor(
+                out=hg[:],
+                in0=hs[:],
+                in1=g1_t[:, u, :].unsqueeze(1).to_broadcast([P, 256, PACK]),
+                op=ALU.mult,
+            )
+            return hg
+
+        def gain1_pe(c0, u):
+            bank = psum.tile([P, PACK, 256], BF16, name="by", bufs=4)
+            for j in range(PACK):
+                nc.tensor.matmul(
+                    out=bank[:, j, :],
+                    lhsT=diag[:, u, j, :],
+                    rhs=h_raw[:, j, c0 - u : c0 - u + 256],
+                    start=True,
+                    stop=True,
+                )
+            hg = work.tile([P, 256, PACK], BF16, name="hgp", align_bytes=64, bufs=4)
+            nc.scalar.copy(out=hg[:], in_=bank[:].rearrange("p j c -> p c j"))
+            return hg
 
         fin = {}
         for half in range(2):
@@ -310,162 +337,147 @@ def tile_convolutivenmfexponentiatedupdate_x2_kernel(
                     in_=pcs[half][1][32 * x : 32 * x + 4, :].bitcast(I32),
                 )
 
-        diag = keep.tile([P, 3, PACK, P], F32, name="diag")
-        for u in range(1, TAPS):
-            for j in range(PACK):
-                nc.gpsimd.tensor_scalar(
-                    out=diag[:, u - 1, j, :], in0=ident[:], scalar1=g2_t[:, u, j : j + 1],
-                    scalar2=0.0, op0=ALU.mult, op1=ALU.add)
-
         vcopy = nc.vector.tensor_copy
         scopy = nc.scalar.copy
-        lay(vcopy, h_int, 3 + 240, h_raw, 240, 416)
-        lay(scopy, h_int, 3 + 416, h_raw, 416, 512)
-        lay(scopy, h_int, 3, h_raw, 0, 128)
-        lay(scopy, h_int, 3 + 128, h_raw, 128, 240)
-        lay(scopy, h_int, 0, h_raw, T - 3, T)
-        for i in range(4):
-            lay(scopy, h_int, 515 + 128 * i, h_raw, 512 + 128 * i, 640 + 128 * i)
-        for i in range(8):
-            lay(scopy, v_int, 128 * i, v_raw, 128 * i, 128 * i + 128)
+        for u in range(TAPS):
+            for j in range(PACK):
+                nc.vector.tensor_scalar(
+                    out=diag[:, u, j, :], in0=ident_b[:], scalar1=g1_t[:, u, j : j + 1],
+                    scalar2=None, op0=ALU.mult)
+        hp = [gain1_pe(768, u) for u in range(3)] + [gain1_pe(512, u) for u in range(4)]
+
+        def qa(hg):
+            return quant(hg, 256, "hqa", 256, 8)
 
         s_a = banks_of("bx")
-        qs = []
-        hg = [gain1(256, 256, 0), gain1(256, 256, 1)]
-        for u in range(TAPS):
-            qs.append(quant(hg[u], 256, "hqa", 256, 8))
-            if u + 2 < TAPS:
-                hg.append(gain1(256, 256, u + 2))
-        h2 = [gain1(0, 256, 0), gain1(0, 256, 1)]
+        v1 = gain1_v(768, 3)
+        k0 = qa(hp[0])
+        k3 = qa(v1)
+        lay(vcopy, h_int, 3, h_raw, 0, 128)
+        k1 = qa(hp[1])
         permute_scales()
         permute_words(0)
-        mm1(s_a, 256, 256, 0, qs[0])
+        mm1(s_a, 256, 256, 0, k0, True, False)
         permute_words(1)
-        mm1(s_a, 256, 256, 1, qs[1])
+        mm1(s_a, 256, 256, 1, k1, False, False)
+        k2 = qa(hp[2])
         permute_words(2)
-        mm1(s_a, 256, 256, 2, qs[2])
+        mm1(s_a, 256, 256, 2, k2, False, False)
         permute_words(3)
-        mm1(s_a, 256, 256, 3, qs[3])
-        for u in range(TAPS):
-            q = quant(h2[u], 256, "hqa", 256, 8)
-            if u + 2 < TAPS:
-                h2.append(gain1(0, 256, u + 2))
-            mm1(s_a, 0, 256, u, q)
-
-        for j in range(PACK):
-            exp1(0, s_a, j)
-        for j in range(PACK):
-            ln1(0, j)
-
+        mm1(s_a, 256, 256, 3, k3, False, True)
+        mm1(s_a, 0, 256, 0, qa(hp[3]), True, False)
+        lay(vcopy, h_int, 3 + 128, h_raw, 128, 256)
+        mm1(s_a, 0, 256, 1, qa(hp[4]), False, False)
+        lay(vcopy, h_int, 3 + 256, h_raw, 256, 384)
+        lay(vcopy, h_int, 3 + 384, h_raw, 384, 512)
+        mm1(s_a, 0, 256, 2, qa(hp[5]), False, False)
+        lay(vcopy, h_int, 0, h_raw, T - 3, T)
+        mm1(s_a, 0, 256, 3, qa(hp[6]), False, True)
         s_b = banks_of("by")
+        hb = [gain1(0), gain1(1)]
 
-        def soft_a(j):
-            softplus(0, s_a, j)
-            ln2(0, j)
+        def qb(u):
+            q = quant(hb[u], HALF, "hq", HALF, 4)
+            mm1(s_b, 0, 512, u, q, u == 0, u == 3)
 
-        def soft_b(j):
-            softplus(1, s_b, j)
-            ln2(1, j)
-
-        stage1_unit(
-            s_b, 512, 512,
-            {2: [lambda: soft_a(0), lambda: soft_a(1)], 3: [lambda: soft_a(2), lambda: soft_a(3)]},
-        )
-        nc.vector.tensor_scalar(
-            out=mu_b[:], in0=mu_t[:, :, 0], scalar1=-0.5, scalar2=None, op0=ALU.mult
-        )
-        rs = [exp2(i) for i in range(4)]
         for j in range(PACK):
-            exp1(1, s_b, j)
+            exp1(1, s_a, j)
         for j in range(PACK):
             ln1(1, j)
 
+        def soft_a(j):
+            softplus(1, s_a, j)
+            ln2(1, j)
+
+        def soft_b(j):
+            softplus(0, s_b, j)
+            ln2(0, j)
+
+        qb(0)
+        hb.append(gain1(2))
+        qb(1)
+        hb.append(gain1(3))
+        qb(2)
+        soft_a(0)
+        soft_a(1)
+        qb(3)
+        soft_a(2)
+        soft_a(3)
+        lay(vcopy, v_int, 512, v_raw, 512, 768)
+        lay(vcopy, v_int, 768, v_raw, 768, 1024)
+        nc.vector.tensor_scalar(
+            out=mu_b[:], in0=mu_t[:, :, 0], scalar1=-0.5, scalar2=None, op0=ALU.mult
+        )
+        nc.vector.tensor_copy(out=g2f[:], in_=g2_t[:])
+        nc.vector.tensor_scalar(out=ng2f[:], in0=g2_t[:], scalar1=-1.0, scalar2=None, op0=ALU.mult)
+        lay(vcopy, v_int, 0, v_raw, 0, 256)
+        rs = [exp2(i) for i in range(4, 8)]
+        for j in range(PACK):
+            exp1(0, s_b, j)
+        for j in range(PACK):
+            ln1(0, j)
+
+        def mmq(banks, off, width, u, eg, first=None, last=None):
+            mm2(banks, off, width, u, quant(eg, width, "eq", 256, 8), first, last)
+
         r_a = banks_of("bx")
+        ratio(4, rs[0])
+        ratio(5, rs[1])
+        stage2_unit(r_a, 512, 128, {})
+        ratio(6, rs[2])
+        ratio(7, rs[3])
+        stage2_unit(r_a, 640, 256, {0: [lambda j=j: soft_b(j) for j in range(4)]})
+        lay(vcopy, v_int, 256, v_raw, 256, 512)
+        rs = [exp2(i) for i in range(4)]
+        r_b = banks_of("bx")
+        ex_a = {}
+
+        def out_a(m):
+            fround(scopy, fmul(ex_a[m], m, HALF, HALF), m, HALF, HALF)
+
         ratio(0, rs[0])
         vcopy(out=e_int[:, T : T + 3, :], in_=e_int[:, 0:3, :])
         ratio(1, rs[1])
-        stage2_unit(r_a, 0, 128, {})
+        stage2_unit(r_a, 896, 128, {})
+        for m in range(4):
+            ex_a[m] = fexp(r_a, m, HALF, HALF)
         ratio(2, rs[2])
         ratio(3, rs[3])
-        stage2_unit(
-            r_a, 128, 256,
-            {0: [lambda: soft_b(0), lambda: soft_b(1), lambda: soft_b(2), lambda: soft_b(3)]},
-        )
-        rs = [exp2(i) for i in range(4, 8)]
-        r_b = banks_of("bx")
-        for i in range(4):
-            ratio(4 + i, rs[i])
-        em1 = keep.tile([P, 260, PACK], F32, name="em1")
-        for a, b in ((0, 131), (131, 260)):
-            nc.scalar.activation(
-                out=em1[:, a:b, :], in_=e_int[:, 640 + a : 640 + b, :], func=ACT.Identity, bias=-1.0
-            )
-        pe_eg = {}
-
-        def gain2_pe(u):
-            eg = work.tile([P, 256, PACK], BF16, name="egp", align_bytes=64, bufs=4)
-            for i in range(2):
-                bank = bank_of("by")
-                for j in range(PACK):
-                    nc.tensor.matmul(
-                        out=bank[:, j * P : (j + 1) * P],
-                        lhsT=diag[:, u - 1, j, :],
-                        rhs=em1[:, i * P + u : (i + 1) * P + u, j],
-                        start=True,
-                        stop=True,
-                    )
-                nc.scalar.copy(
-                    out=eg[:, i * P : (i + 1) * P, :],
-                    in_=bank[:].rearrange("p (j c) -> p c j", j=PACK),
-                )
-            pe_eg[u] = eg
-
-        ex_a = {}
-
-        def out_a(m, eng):
-            fround(eng, fmul(ex_a[m], m, 0, HALF), m, 0, HALF)
-
-        def mmq(banks, off, width, u, eg):
-            mm2(banks, off, width, u, quant(eg, width, "eq", 256, 8))
-
-        eg = [gain2(384, 128, u) for u in range(TAPS)]
-        gain2_pe(1)
-        for u in range(TAPS):
-            mmq(r_a, 384, 128, u, eg[u])
+        s3 = gain2_s(128, 256, 3)
+        stage2_unit(r_b, 0, 128, {})
+        s7 = gain2_s(384, 128, 3)
+        e = [gain2(128, 256, 0)]
+        out_a(0)
+        e.append(gain2(128, 256, 1))
+        out_a(1)
+        mmq(r_b, 128, 256, 0, e[0])
+        out_a(2)
+        mmq(r_b, 128, 256, 1, e[1])
+        out_a(3)
+        e.append(gain2(128, 256, 2))
+        mmq(r_b, 128, 256, 3, s3, False, False)
+        mmq(r_b, 128, 256, 2, e[2], False, True)
+        pin_a = [pinlay(scopy, turn(1, k)) for k in range(2)]
+        ex_b = [fexp(r_b, m, 0, 384) for m in range(4)]
+        e7 = [gain2(384, 128, u) for u in range(3)]
+        mmq(r_b, 384, 128, 0, e7[0])
+        mmq(r_b, 384, 128, 1, e7[1])
+        mmq(r_b, 384, 128, 3, s7, False, False)
+        mmq(r_b, 384, 128, 2, e7[2], False, True)
+        ex_c = [fexp(r_b, m, 384, 128) for m in range(4)]
+        for k in range(2):
+            planes(1, k, pin_a[k])
+        scales_out(1)
+        res = [fmul(ex_b[m], m, 0, 384) for m in range(4)]
         for m in range(4):
-            ex_a[m] = fexp(r_a, m, 0, HALF)
-        gain2_pe(2)
-        eg = [gain2(512, 128, u) for u in range(TAPS)]
-        for u in range(TAPS):
-            mmq(r_b, 0, 128, u, eg[u])
-        gain2_pe(3)
-        out_a(0, scopy)
-        mmq(r_b, 128, 256, 0, gain2(640, 256, 0))
-        out_a(1, scopy)
-        mmq(r_b, 128, 256, 1, pe_eg[1])
-
-        out_a(2, scopy)
-        out_a(3, scopy)
-        mmq(r_b, 128, 256, 2, pe_eg[2])
-        e7 = [gain2(896, 128, u) for u in range(TAPS)]
-        mmq(r_b, 128, 256, 3, pe_eg[3])
-        ex_b = [fexp(r_b, m, 512, 384) for m in range(4)]
-        for u in range(TAPS):
-            mmq(r_b, 384, 128, u, e7[u])
-        pin_a = [pinlay(scopy, turn(0, k)) for k in range(2)]
-        res = [fmul(ex_b[m], m, 512, 384) for m in range(4)]
-        ex_c = [fexp(r_b, m, 896, 128) for m in range(4)]
-        for m in range(4):
-            fround(scopy if m % 2 else vcopy, res[m], m, 512, 384)
-        planes(0, 0, pin_a[0])
-        planes(0, 1, pin_a[1])
-        scales_out(0)
+            fround(scopy, res[m], m, 0, 384)
         p = [None, None]
         for k in range(2):
-            res = [fmul(ex_c[m], m, 896, 128) for m in (2 * k, 2 * k + 1)]
+            res = [fmul(ex_c[m], m, 384, 128) for m in (2 * k, 2 * k + 1)]
             for i in range(2):
-                fround(vcopy, res[i], 2 * k + i, 896, 128)
-            p[k] = pinlay(scopy if k == 0 else vcopy, turn(1, k))
-        planes(1, 0, p[0])
-        planes(1, 1, p[1])
-        scales_out(1)
+                fround(vcopy, res[i], 2 * k + i, 384, 128)
+        for k in range(2):
+            p[k] = pinlay(scopy if k == 0 else vcopy, turn(0, k))
+        planes(0, 0, p[0])
+        planes(0, 1, p[1])
+        scales_out(0)

@@ -57,7 +57,7 @@ def tile_convolutivenmfexponentiatedupdate_x2_kernel(
         h_pj = h.rearrange("(p j) t -> p j t", j=PACK)
         v_pj = v.rearrange("(p j) t -> p j t", j=PACK)
         nc.scalar.dma_start(out=g1_t[:], in_=g1.rearrange("(u p j) -> p u j", u=TAPS, j=PACK))
-        for a, b in ((752, T), (496, 752), (0, 496)):
+        for a, b in ((752, T), (496, 752)):
             nc.sync.dma_start(out=h_raw[:, :, a:b], in_=h_pj[:, :, a:b])
         nc.vector.memset(warm[:], 0.0)
         nc.vector.memset(w1s_raw[:].bitcast(I32), 0)
@@ -74,12 +74,9 @@ def tile_convolutivenmfexponentiatedupdate_x2_kernel(
             nc.sync.dma_start(
                 out=w1w_raw[:, u, :], in_=w1_words[u].rearrange("p n b -> p (n b)").bitcast(I32)
             )
+        nc.sync.dma_start(out=h_raw[:, :, 0:496], in_=h_pj[:, :, 0:496])
         for a in (HALF, 0):
             nc.sync.dma_start(out=v_raw[:, :, a : a + HALF], in_=v_pj[:, :, a : a + HALF])
-        nc.gpsimd.dma_start(out=g2_t[:], in_=g2.rearrange("(u p j) -> p u j", u=TAPS, j=PACK))
-        nc.gpsimd.dma_start(
-            out=mu_t[:, :, 0:1], in_=mu.rearrange("(m p o) -> p m o", m=4, o=1)
-        )
         for q in range(4):
             nc.sync.dma_start(
                 out=w2s[32 * q : 32 * q + 16, :].bitcast(I32),
@@ -89,12 +86,21 @@ def tile_convolutivenmfexponentiatedupdate_x2_kernel(
             nc.sync.dma_start(
                 out=w2w[:, u, :], in_=w2_words[u].rearrange("p n b -> p (n b)").bitcast(I32)
             )
+        nc.sync.dma_start(out=g2_t[:], in_=g2.rearrange("(u p j) -> p u j", u=TAPS, j=PACK))
+        nc.sync.dma_start(out=mu_t[:, :, 0:1], in_=mu.rearrange("(m p o) -> p m o", m=4, o=1))
         nc.sync.dma_start(out=h_nat[:], in_=h.rearrange("(m p) t -> p m t", p=P))
 
         def lay(engine_copy, dst, dst0, src, a, b):
-            engine_copy(
-                out=dst[:, dst0 : dst0 + b - a, :], in_=src[:, :, a:b].rearrange("p j c -> p c j")
-            )
+            if (b - a) % 4:
+                engine_copy(
+                    out=dst[:, dst0 : dst0 + b - a, :],
+                    in_=src[:, :, a:b].rearrange("p j c -> p c j"),
+                )
+            else:
+                engine_copy(
+                    out=dst[:, dst0 : dst0 + b - a, :].rearrange("p (c i) j -> p c j i", i=4),
+                    in_=src[:, :, a:b].rearrange("p j (c i) -> p c j i", i=4),
+                )
 
         def gain1(u):
             hg = work.tile([P, HALF, PACK], BF16, name="hg", align_bytes=64, bufs=3)
@@ -175,8 +181,8 @@ def tile_convolutivenmfexponentiatedupdate_x2_kernel(
         def exp2(i):
             r = work.tile([P, P, PACK], F32, name="r", bufs=4)
             nc.scalar.activation(
-                out=r[:],
-                in_=lg[:, :, i * P : (i + 1) * P].rearrange("p j c -> p c j"),
+                out=r[:].rearrange("p (c i) j -> p c j i", i=4),
+                in_=lg[:, :, i * P : (i + 1) * P].rearrange("p j (c i) -> p c j i", i=4),
                 func=ACT.Exp,
                 scale=-1.0,
             )
@@ -215,6 +221,65 @@ def tile_convolutivenmfexponentiatedupdate_x2_kernel(
                     start=first,
                     stop=last,
                 )
+
+        def pair2(a, u):
+            eg = work.tile([P, 2, P, PACK], BF16, name="egq", align_bytes=64, bufs=3)
+            for i in range(2):
+                nc.vector.scalar_tensor_tensor(
+                    out=eg[:, i, :, :],
+                    in0=e_int[:, a + u + i : a + u + i + P, :],
+                    scalar=-1.0,
+                    in1=g2_t[:, u + i, :].unsqueeze(1).to_broadcast([P, P, PACK]),
+                    op0=ALU.add,
+                    op1=ALU.mult,
+                )
+            return eg
+
+        def pair2_s(a, u):
+            eg = work.tile([P, 2, P, PACK], BF16, name="egt", align_bytes=64, bufs=2)
+            for i in range(2):
+                for j in range(PACK):
+                    nc.scalar.activation(
+                        out=eg[:, i, :, j],
+                        in_=e_int[:, a + u + i : a + u + i + P, j],
+                        func=ACT.Identity,
+                        scale=g2f[:, u + i, j : j + 1],
+                        bias=ng2f[:, u + i, j : j + 1],
+                    )
+            return eg
+
+        def single_s(a, u):
+            eg = work.tile([P, 2, P, PACK], BF16, name="egt", align_bytes=64, bufs=2)
+            for j in range(PACK):
+                nc.scalar.activation(
+                    out=eg[:, 1, :, j],
+                    in_=e_int[:, a + u : a + u + P, j],
+                    func=ACT.Identity,
+                    scale=g2f[:, u, j : j + 1],
+                    bias=ng2f[:, u, j : j + 1],
+                )
+            return eg
+
+        def pair_first(a, u, eg):
+            nc.vector.scalar_tensor_tensor(
+                out=eg[:, 0, :, :],
+                in0=e_int[:, a + u : a + u + P, :],
+                scalar=-1.0,
+                in1=g2_t[:, u, :].unsqueeze(1).to_broadcast([P, P, PACK]),
+                op0=ALU.add,
+                op1=ALU.mult,
+            )
+            return eg
+
+        def pairq(banks, off, u, eg):
+            codes = work.tile([P, 256], U32, name="eq_c", align_bytes=64, bufs=8)
+            scales = work.tile([P, 256], U8, name="eq_s", align_bytes=64, bufs=8)
+            nc.vector.quantize_mx(
+                out=codes[:].bitcast(FP8X4), scales=scales[:], in_=eg[:].rearrange("p i c j -> p (i c j)")
+            )
+            for i in range(2):
+                at = slice(i * P, (i + 1) * P)
+                mm2(banks, off, P, u + i, (codes[:, at], scales[:, at]))
 
         def stage2_unit(banks, a, width, between):
             off = a % HALF
@@ -353,25 +418,25 @@ def tile_convolutivenmfexponentiatedupdate_x2_kernel(
         v1 = gain1_v(768, 3)
         k0 = qa(hp[0])
         k3 = qa(v1)
-        lay(vcopy, h_int, 3, h_raw, 0, 128)
-        k1 = qa(hp[1])
         permute_scales()
         permute_words(0)
         mm1(s_a, 256, 256, 0, k0, True, False)
+        k1 = qa(hp[1])
         permute_words(1)
         mm1(s_a, 256, 256, 1, k1, False, False)
-        k2 = qa(hp[2])
         permute_words(2)
+        k2 = qa(hp[2])
         mm1(s_a, 256, 256, 2, k2, False, False)
         permute_words(3)
         mm1(s_a, 256, 256, 3, k3, False, True)
         mm1(s_a, 0, 256, 0, qa(hp[3]), True, False)
+        lay(vcopy, h_int, 0, h_raw, T - 3, T)
+        lay(vcopy, h_int, 3, h_raw, 0, 128)
         lay(vcopy, h_int, 3 + 128, h_raw, 128, 256)
         mm1(s_a, 0, 256, 1, qa(hp[4]), False, False)
         lay(vcopy, h_int, 3 + 256, h_raw, 256, 384)
         lay(vcopy, h_int, 3 + 384, h_raw, 384, 512)
         mm1(s_a, 0, 256, 2, qa(hp[5]), False, False)
-        lay(vcopy, h_int, 0, h_raw, T - 3, T)
         mm1(s_a, 0, 256, 3, qa(hp[6]), False, True)
         s_b = banks_of("by")
         hb = [gain1(0), gain1(1)]
@@ -411,6 +476,7 @@ def tile_convolutivenmfexponentiatedupdate_x2_kernel(
         nc.vector.tensor_copy(out=g2f[:], in_=g2_t[:])
         nc.vector.tensor_scalar(out=ng2f[:], in0=g2_t[:], scalar1=-1.0, scalar2=None, op0=ALU.mult)
         lay(vcopy, v_int, 0, v_raw, 0, 256)
+        lay(vcopy, v_int, 256, v_raw, 256, 512)
         rs = [exp2(i) for i in range(4, 8)]
         for j in range(PACK):
             exp1(0, s_b, j)
@@ -423,11 +489,12 @@ def tile_convolutivenmfexponentiatedupdate_x2_kernel(
         r_a = banks_of("bx")
         ratio(4, rs[0])
         ratio(5, rs[1])
-        stage2_unit(r_a, 512, 128, {})
+        eg = [pair2(512, 0), pair2(512, 2)]
+        pairq(r_a, 0, 0, eg[0])
         ratio(6, rs[2])
+        pairq(r_a, 0, 2, eg[1])
         ratio(7, rs[3])
         stage2_unit(r_a, 640, 256, {0: [lambda j=j: soft_b(j) for j in range(4)]})
-        lay(vcopy, v_int, 256, v_raw, 256, 512)
         rs = [exp2(i) for i in range(4)]
         r_b = banks_of("bx")
         ex_a = {}
@@ -436,48 +503,58 @@ def tile_convolutivenmfexponentiatedupdate_x2_kernel(
             fround(scopy, fmul(ex_a[m], m, HALF, HALF), m, HALF, HALF)
 
         ratio(0, rs[0])
-        vcopy(out=e_int[:, T : T + 3, :], in_=e_int[:, 0:3, :])
         ratio(1, rs[1])
-        stage2_unit(r_a, 896, 128, {})
+        vcopy(out=e_int[:, T : T + 3, :], in_=e_int[:, 0:3, :])
+        eg = [pair2(896, 0), pair2(896, 2)]
+        s01 = pair2_s(0, 2)
+        pairq(r_a, 384, 0, eg[0])
+        ratio(2, rs[2])
+        pairq(r_a, 384, 2, eg[1])
+        ratio(3, rs[3])
         for m in range(4):
             ex_a[m] = fexp(r_a, m, HALF, HALF)
-        ratio(2, rs[2])
-        ratio(3, rs[3])
         s3 = gain2_s(128, 256, 3)
-        stage2_unit(r_b, 0, 128, {})
-        s7 = gain2_s(384, 128, 3)
+        eg = [pair2(0, 0)]
         e = [gain2(128, 256, 0)]
-        out_a(0)
+        pairq(r_b, 0, 0, eg[0])
         e.append(gain2(128, 256, 1))
+        pairq(r_b, 0, 2, s01)
+        out_a(0)
         out_a(1)
         mmq(r_b, 128, 256, 0, e[0])
         out_a(2)
         mmq(r_b, 128, 256, 1, e[1])
         out_a(3)
+        s7 = single_s(384, 3)
         e.append(gain2(128, 256, 2))
         mmq(r_b, 128, 256, 3, s3, False, False)
         mmq(r_b, 128, 256, 2, e[2], False, True)
-        pin_a = [pinlay(scopy, turn(1, k)) for k in range(2)]
         ex_b = [fexp(r_b, m, 0, 384) for m in range(4)]
-        e7 = [gain2(384, 128, u) for u in range(3)]
-        mmq(r_b, 384, 128, 0, e7[0])
-        mmq(r_b, 384, 128, 1, e7[1])
-        mmq(r_b, 384, 128, 3, s7, False, False)
-        mmq(r_b, 384, 128, 2, e7[2], False, True)
+        turned = [turn(1, k) for k in range(2)]
+        eg = [pair2(384, 0)]
+        pairq(r_b, 384, 0, eg[0])
+        half = pair_first(384, 2, s7)
+        pairq(r_b, 384, 2, half)
         ex_c = [fexp(r_b, m, 384, 128) for m in range(4)]
+        res = [fmul(ex_b[m], m, 0, 384) for m in range(4)]
+        for m in range(2):
+            fround(scopy, res[m], m, 0, 384)
+        pin_a = [pinlay(scopy, turned[k]) for k in range(2)]
+        last = [fmul(ex_c[m], m, 384, 128) for m in range(2)]
+        for m in range(2):
+            fround(vcopy, last[m], m, 384, 128)
+        b0 = turn(0, 0)
+        last = [fmul(ex_c[m], m, 384, 128) for m in (2, 3)]
+        for m in (2, 3):
+            fround(vcopy, res[m], m, 0, 384)
+        for m in (2, 3):
+            fround(vcopy, last[m - 2], m, 384, 128)
+        b1 = turn(0, 1)
+        p0 = pinlay(scopy, b0)
         for k in range(2):
             planes(1, k, pin_a[k])
         scales_out(1)
-        res = [fmul(ex_b[m], m, 0, 384) for m in range(4)]
-        for m in range(4):
-            fround(scopy, res[m], m, 0, 384)
-        p = [None, None]
-        for k in range(2):
-            res = [fmul(ex_c[m], m, 384, 128) for m in (2 * k, 2 * k + 1)]
-            for i in range(2):
-                fround(vcopy, res[i], 2 * k + i, 384, 128)
-        for k in range(2):
-            p[k] = pinlay(scopy if k == 0 else vcopy, turn(0, k))
-        planes(0, 0, p[0])
-        planes(0, 1, p[1])
+        p1 = pinlay(vcopy, b1)
+        planes(0, 0, p0)
+        planes(0, 1, p1)
         scales_out(0)

@@ -36,7 +36,7 @@ def tile_convolutivenmfexponentiatedupdate_x2_kernel(
         mu_t = keep.tile([P, 4, 2], BF16, name="mu_t")
         mu_b = keep.tile([P, 4], F32, name="mu_b")
         h_raw = keep.tile([P, PACK, T], BF16, name="h_raw")
-        h_int = keep.tile([P, 3 + HALF, PACK], BF16, name="h_int")
+        h_int = keep.tile([P, 4 + HALF, PACK], BF16, name="h_int")
         h_nat = keep.tile([P, 4, T], BF16, name="h_nat")
         v_raw = keep.tile([P, PACK, T], BF16, name="v_raw")
         v_int = keep.tile([P, T, PACK], BF16, name="v_int")
@@ -104,7 +104,7 @@ def tile_convolutivenmfexponentiatedupdate_x2_kernel(
 
         def gain1(u):
             hg = work.tile([P, HALF, PACK], BF16, name="hg", align_bytes=64, bufs=3)
-            a = 3 - u
+            a = 4 - u
             nc.vector.tensor_tensor(
                 out=hg[:],
                 in0=h_int[:, a : a + HALF, :],
@@ -430,12 +430,12 @@ def tile_convolutivenmfexponentiatedupdate_x2_kernel(
         permute_words(3)
         mm1(s_a, 256, 256, 3, k3, False, True)
         mm1(s_a, 0, 256, 0, qa(hp[3]), True, False)
-        lay(vcopy, h_int, 0, h_raw, T - 3, T)
-        lay(vcopy, h_int, 3, h_raw, 0, 128)
-        lay(vcopy, h_int, 3 + 128, h_raw, 128, 256)
+        lay(vcopy, h_int, 1, h_raw, T - 3, T)
+        lay(vcopy, h_int, 4, h_raw, 0, 128)
+        lay(vcopy, h_int, 4 + 128, h_raw, 128, 256)
         mm1(s_a, 0, 256, 1, qa(hp[4]), False, False)
-        lay(vcopy, h_int, 3 + 256, h_raw, 256, 384)
-        lay(vcopy, h_int, 3 + 384, h_raw, 384, 512)
+        lay(vcopy, h_int, 4 + 256, h_raw, 256, 384)
+        lay(vcopy, h_int, 4 + 384, h_raw, 384, 512)
         mm1(s_a, 0, 256, 2, qa(hp[5]), False, False)
         mm1(s_a, 0, 256, 3, qa(hp[6]), False, True)
         s_b = banks_of("by")
@@ -525,16 +525,14 @@ def tile_convolutivenmfexponentiatedupdate_x2_kernel(
         out_a(2)
         mmq(r_b, 128, 256, 1, e[1])
         out_a(3)
-        s7 = single_s(384, 3)
         e.append(gain2(128, 256, 2))
         mmq(r_b, 128, 256, 3, s3, False, False)
         mmq(r_b, 128, 256, 2, e[2], False, True)
         ex_b = [fexp(r_b, m, 0, 384) for m in range(4)]
         turned = [turn(1, k) for k in range(2)]
-        eg = [pair2(384, 0)]
+        eg = [pair2(384, 0), pair2(384, 2)]
         pairq(r_b, 384, 0, eg[0])
-        half = pair_first(384, 2, s7)
-        pairq(r_b, 384, 2, half)
+        pairq(r_b, 384, 2, eg[1])
         ex_c = [fexp(r_b, m, 384, 128) for m in range(4)]
         res = [fmul(ex_b[m], m, 0, 384) for m in range(4)]
         for m in range(2):

from contextlib import ExitStack

import concourse.mybir as mybir
from concourse.masks import make_identity

F32 = mybir.dt.float32
BF16 = mybir.dt.bfloat16
I32 = mybir.dt.int32
U32 = mybir.dt.uint32
U8 = mybir.dt.uint8
FP8X4 = mybir.dt.float8_e4m3fn_x4
ACT = mybir.ActivationFunctionType
ALU = mybir.AluOpType

P = 128
TAPS = 4
PACK = 4
T = 1024
HALF = 512
FLOPS = 2 * 2 * 512 * 2048 * 1024


def tile_convolutivenmfexponentiatedupdate_x2_kernel(
    tc, v, h, w1_words, w1_scales, g1, w2_words, w2_scales, g2, mu, out_0, out_1, out_2
):
    nc = tc.nc
    with ExitStack() as ctx:
        keep = ctx.enter_context(tc.tile_pool(name="keep", bufs=1))
        work = ctx.enter_context(tc.tile_pool(name="work", bufs=3))
        psum = ctx.enter_context(tc.psum_pool(name="psum", bufs=4))
        ctx.enter_context(tc.manual_schedule())

        warm = keep.tile([P, 1], F32, name="warm")
        g1_t = keep.tile([P, TAPS, PACK], BF16, name="g1_t")
        g2_t = keep.tile([P, TAPS, PACK], BF16, name="g2_t")
        mu_t = keep.tile([P, 4, 2], BF16, name="mu_t")
        mu_b = keep.tile([P, 4], F32, name="mu_b")
        h_raw = keep.tile([P, PACK, T], BF16, name="h_raw")
        h_int = keep.tile([P, 4 + HALF, PACK], BF16, name="h_int")
        h_nat = keep.tile([P, 4, T], BF16, name="h_nat")
        v_raw = keep.tile([P, PACK, T], BF16, name="v_raw")
        v_int = keep.tile([P, T, PACK], BF16, name="v_int")
        w1w_raw = keep.tile([P, TAPS, 512], I32, name="w1w_raw")
        w1w = keep.tile([P, TAPS, PACK, P], I32, name="w1w", align_bytes=64)
        w1s_raw = keep.tile([P, 512], U8, name="w1s_raw", align_bytes=64)
        w1s = keep.tile([P, PACK, P], U8, name="w1s", align_bytes=64)
        w2w = keep.tile([P, TAPS, 512], I32, name="w2w", align_bytes=64)
        w2s = keep.tile([P, 512], U8, name="w2s", align_bytes=64)
        ident = keep.tile([P, P], F32, name="ident")
        ident_b = keep.tile([P, P], BF16, name="ident_b")
        diag = keep.tile([P, TAPS, PACK, P], BF16, name="diag")
        g2f = keep.tile([P, TAPS, PACK], F32, name="g2f")
        ng2f = keep.tile([P, TAPS, PACK], F32, name="ng2f")
        lg = keep.tile([P, PACK, T], F32, name="lg")
        e_int = keep.tile([P, T + 3, PACK], F32, name="e_int")

        h_pj = h.rearrange("(p j) t -> p j t", j=PACK)
        v_pj = v.rearrange("(p j) t -> p j t", j=PACK)
        nc.scalar.dma_start(out=g1_t[:], in_=g1.rearrange("(u p j) -> p u j", u=TAPS, j=PACK))
        for a, b in ((752, T), (496, 752)):
            nc.sync.dma_start(out=h_raw[:, :, a:b], in_=h_pj[:, :, a:b])
        nc.vector.memset(warm[:], 0.0)
        nc.vector.memset(w1s_raw[:].bitcast(I32), 0)
        nc.vector.memset(w2s[:].bitcast(I32), 0)
        nc.scalar.activation(out=warm[:], in_=warm[:], func=ACT.Exp)
        make_identity(nc, ident_b[:])
        make_identity(nc, ident[:])
        for q in range(4):
            nc.sync.dma_start(
                out=w1s_raw[32 * q : 32 * q + 16, :].bitcast(I32),
                in_=w1_scales[:, 4 * q : 4 * q + 4, :].bitcast(I32),
            )
        for u in range(TAPS):
            nc.sync.dma_start(
                out=w1w_raw[:, u, :], in_=w1_words[u].rearrange("p n b -> p (n b)").bitcast(I32)
            )
        nc.sync.dma_start(out=h_raw[:, :, 0:496], in_=h_pj[:, :, 0:496])
        for a in (HALF, 0):
            nc.sync.dma_start(out=v_raw[:, :, a : a + HALF], in_=v_pj[:, :, a : a + HALF])
        for q in range(4):
            nc.sync.dma_start(
                out=w2s[32 * q : 32 * q + 16, :].bitcast(I32),
                in_=w2_scales[:, 4 * q : 4 * q + 4, :].bitcast(I32),
            )
        for u in range(TAPS):
            nc.sync.dma_start(
                out=w2w[:, u, :], in_=w2_words[u].rearrange("p n b -> p (n b)").bitcast(I32)
            )
        nc.sync.dma_start(out=g2_t[:], in_=g2.rearrange("(u p j) -> p u j", u=TAPS, j=PACK))
        nc.sync.dma_start(out=mu_t[:, :, 0:1], in_=mu.rearrange("(m p o) -> p m o", m=4, o=1))
        nc.sync.dma_start(out=h_nat[:], in_=h.rearrange("(m p) t -> p m t", p=P))

        def lay(engine_copy, dst, dst0, src, a, b):
            if (b - a) % 4:
                engine_copy(
                    out=dst[:, dst0 : dst0 + b - a, :],
                    in_=src[:, :, a:b].rearrange("p j c -> p c j"),
                )
            else:
                engine_copy(
                    out=dst[:, dst0 : dst0 + b - a, :].rearrange("p (c i) j -> p c j i", i=4),
                    in_=src[:, :, a:b].rearrange("p j (c i) -> p c j i", i=4),
                )

        def gain1(u):
            hg = work.tile([P, HALF, PACK], BF16, name="hg", align_bytes=64, bufs=3)
            a = 4 - u
            nc.vector.tensor_tensor(
                out=hg[:],
                in0=h_int[:, a : a + HALF, :],
                in1=g1_t[:, u, :].unsqueeze(1).to_broadcast([P, HALF, PACK]),
                op=ALU.mult,
            )
            return hg

        def quant(src, width, name, cols, bufs):
            codes = work.tile([P, cols], U32, name=name + "_c", align_bytes=64, bufs=bufs)
            scales = work.tile([P, cols], U8, name=name + "_s", align_bytes=64, bufs=bufs)
            nc.vector.quantize_mx(
                out=codes[:, 0:width].bitcast(FP8X4),
                scales=scales[:, 0:width],
                in_=src[:, 0:width, :].rearrange("p c j -> p (c j)"),
            )
            return codes, scales

        def mm1(banks, off, width, u, q, first, last):
            for j in range(PACK):
                nc.tensor.matmul_mx(
                    out=banks[j][:, off : off + width],
                    lhsT=w1w[:, u, j, :].bitcast(FP8X4),
                    lhsT_scale=w1s[4 * u : P, j, :],
                    rhs=q[0][:, 0:width].bitcast(FP8X4),
                    rhs_scale=q[1][:, 0:width],
                    start=first,
                    stop=last,
                )

        def permute_words(u):
            nc.vector.tensor_copy(
                out=w1w[:, u, :, :], in_=w1w_raw[:, u, :].rearrange("p (m j) -> p j m", j=PACK)
            )

        def permute_scales():
            nc.vector.tensor_copy(
                out=w1s[:], in_=w1s_raw[:].rearrange("p (m j) -> p j m", j=PACK)
            )

        def bank_of(tag):
            bank = psum.tile([P, HALF], F32, name=tag, bufs=4)
            return bank

        def banks_of(tag):
            return [bank_of(tag) for j in range(4)]

        def cols(half):
            return slice(half * HALF, (half + 1) * HALF)

        def exp1(half, banks, j):
            nc.scalar.activation(out=lg[:, j, cols(half)], in_=banks[j][:], func=ACT.Exp)

        def ln1(half, j):
            nc.scalar.activation(
                out=lg[:, j, cols(half)], in_=lg[:, j, cols(half)], func=ACT.Ln, bias=1.0
            )

        def softplus(half, banks, j):
            nc.vector.scalar_tensor_tensor(
                out=lg[:, j, cols(half)],
                in0=lg[:, j, cols(half)],
                scalar=20.0,
                in1=banks[j][:],
                op0=ALU.min,
                op1=ALU.max,
            )

        def ln2(half, j):
            nc.scalar.activation(
                out=lg[:, j, cols(half)], in_=lg[:, j, cols(half)], func=ACT.Ln, bias=0.25
            )

        def exp2(i):
            r = work.tile([P, P, PACK], F32, name="r", bufs=4)
            nc.scalar.activation(
                out=r[:].rearrange("p (c i) j -> p c j i", i=4),
                in_=lg[:, :, i * P : (i + 1) * P].rearrange("p j (c i) -> p c j i", i=4),
                func=ACT.Exp,
                scale=-1.0,
            )
            return r

        def ratio(i, r):
            nc.vector.tensor_tensor(
                out=e_int[:, i * P : (i + 1) * P, :],
                in0=r[:],
                in1=v_int[:, i * P : (i + 1) * P, :],
                op=ALU.mult,
            )

        def gain2(a, width, u):
            eg = work.tile([P, 256, PACK], BF16, name="eg", align_bytes=64, bufs=6)
            nc.vector.scalar_tensor_tensor(
                out=eg[:, 0:width, :],
                in0=e_int[:, a + u : a + u + width, :],
                scalar=-1.0,
                in1=g2_t[:, u, :].unsqueeze(1).to_broadcast([P, width, PACK]),
                op0=ALU.add,
                op1=ALU.mult,
            )
            return eg

        def mm2(banks, off, width, u, q, first=None, last=None):
            first = u == 0 if first is None else first
            last = u == TAPS - 1 if last is None else last
            for m in range(4):
                nc.tensor.matmul_mx(
                    out=banks[m][:, off : off + width],
                    lhsT=w2w[:, u, m * P : (m + 1) * P].bitcast(FP8X4),
                    lhsT_scale=w2s[4 * u : P, m * P : (m + 1) * P],
                    rhs=q[0][:, 0:width].bitcast(FP8X4),
                    rhs_scale=q[1][:, 0:width],
                    start=first,
                    stop=last,
                )

        def pair2(a, u):
            eg = work.tile([P, 2, P, PACK], BF16, name="egq", align_bytes=64, bufs=3)
            for i in range(2):
                nc.vector.scalar_tensor_tensor(
                    out=eg[:, i, :, :],
                    in0=e_int[:, a + u + i : a + u + i + P, :],
                    scalar=-1.0,
                    in1=g2_t[:, u + i, :].unsqueeze(1).to_broadcast([P, P, PACK]),
                    op0=ALU.add,
                    op1=ALU.mult,
                )
            return eg

        def pair2_s(a, u):
            eg = work.tile([P, 2, P, PACK], BF16, name="egt", align_bytes=64, bufs=2)
            for i in range(2):
                for j in range(PACK):
                    nc.scalar.activation(
                        out=eg[:, i, :, j],
                        in_=e_int[:, a + u + i : a + u + i + P, j],
                        func=ACT.Identity,
                        scale=g2f[:, u + i, j : j + 1],
                        bias=ng2f[:, u + i, j : j + 1],
                    )
            return eg

        def single_s(a, u):
            eg = work.tile([P, 2, P, PACK], BF16, name="egt", align_bytes=64, bufs=2)
            for j in range(PACK):
                nc.scalar.activation(
                    out=eg[:, 1, :, j],
                    in_=e_int[:, a + u : a + u + P, j],
                    func=ACT.Identity,
                    scale=g2f[:, u, j : j + 1],
                    bias=ng2f[:, u, j : j + 1],
                )
            return eg

        def pair_first(a, u, eg):
            nc.vector.scalar_tensor_tensor(
                out=eg[:, 0, :, :],
                in0=e_int[:, a + u : a + u + P, :],
                scalar=-1.0,
                in1=g2_t[:, u, :].unsqueeze(1).to_broadcast([P, P, PACK]),
                op0=ALU.add,
                op1=ALU.mult,
            )
            return eg

        def pairq(banks, off, u, eg):
            codes = work.tile([P, 256], U32, name="eq_c", align_bytes=64, bufs=8)
            scales = work.tile([P, 256], U8, name="eq_s", align_bytes=64, bufs=8)
            nc.vector.quantize_mx(
                out=codes[:].bitcast(FP8X4), scales=scales[:], in_=eg[:].rearrange("p i c j -> p (i c j)")
            )
            for i in range(2):
                at = slice(i * P, (i + 1) * P)
                mm2(banks, off, P, u + i, (codes[:, at], scales[:, at]))

        def stage2_unit(banks, a, width, between):
            off = a % HALF
            eg = {0: gain2(a, width, 0)}
            for u in range(TAPS):
                if u + 1 < TAPS:
                    eg[u + 1] = gain2(a, width, u + 1)
                for f in between.get(u, []):
                    f()
                mm2(banks, off, width, u, quant(eg[u], width, "eq", 256, 8))

        def gain2_s(a, width, u):
            eg = work.tile([P, 256, PACK], BF16, name="egs", align_bytes=64, bufs=3)
            for j in range(PACK):
                nc.scalar.activation(
                    out=eg[:, 0:width, j],
                    in_=e_int[:, a + u : a + u + width, j],
                    func=ACT.Identity,
                    scale=g2f[:, u, j : j + 1],
                    bias=ng2f[:, u, j : j + 1],
                )
            return eg

        def gain1_v(c0, u):
            hs = work.tile([P, 256, PACK], BF16, name="hs", bufs=1)
            lay(nc.vector.tensor_copy, hs, 0, h_raw, c0 - u, c0 - u + 256)
            hg = work.tile([P, 256, PACK], BF16, name="hgv", align_bytes=64, bufs=1)
            nc.vector.tensor_tensor(
                out=hg[:],
                in0=hs[:],
                in1=g1_t[:, u, :].unsqueeze(1).to_broadcast([P, 256, PACK]),
                op=ALU.mult,
            )
            return hg

        def gain1_pe(c0, u):
            bank = psum.tile([P, PACK, 256], BF16, name="by", bufs=4)
            for j in range(PACK):
                nc.tensor.matmul(
                    out=bank[:, j, :],
                    lhsT=diag[:, u, j, :],
                    rhs=h_raw[:, j, c0 - u : c0 - u + 256],
                    start=True,
                    stop=True,
                )
            hg = work.tile([P, 256, PACK], BF16, name="hgp", align_bytes=64, bufs=4)
            nc.scalar.copy(out=hg[:], in_=bank[:].rearrange("p j c -> p c j"))
            return hg

        fin = {}
        for half in range(2):
            for m in range(4):
                rb = keep.tile([P, HALF], BF16, name="rb%d%d" % (half, m), align_bytes=64)
                fin[half, m] = rb
        pcs = []
        for half in range(2):
            pc = keep.tile([P, 512], U32, name="pc%d" % half, align_bytes=64)
            ps = keep.tile([P, 512], U8, name="ps%d" % half, align_bytes=64)
            pcs.append((pc, ps))

        def fexp(banks, m, a, width):
            ex = work.tile([P, HALF], F32, name="ex", bufs=6)
            nc.scalar.activation(
                out=ex[:, 0:width],
                in_=banks[m][:, a % HALF : a % HALF + width],
                func=ACT.Exp,
                scale=0.5,
                bias=mu_b[:, m : m + 1],
            )
            return ex

        def fmul(ex, m, a, width):
            res = work.tile([P, HALF], F32, name="res", bufs=8)
            nc.vector.tensor_tensor(
                out=res[:, 0:width], in0=ex[:, 0:width], in1=h_nat[:, m, a : a + width], op=ALU.mult
            )
            nc.sync.dma_start(out=out_0[m * P : (m + 1) * P, a : a + width], in_=res[:, 0:width])
            return res

        def fround(engine_copy, res, m, a, width):
            engine_copy(
                out=fin[a // HALF, m][:, a % HALF : a % HALF + width], in_=res[:, 0:width]
            )

        def turn(half, pair):
            bank = bank_of("by")
            for k in range(2):
                words = fin[half, 2 * pair + k][:].bitcast(F32)
                for x in range(2):
                    base = k * 256 + x * P
                    nc.tensor.transpose(bank[:, base : base + P], words[:, x:256:2], ident[:])
            return bank

        def pinlay(engine_copy, bank):
            pin = work.tile([P, 256, PACK], BF16, name="pin", align_bytes=64)
            engine_copy(
                out=pin[:].rearrange("p k b -> p (k b)").bitcast(F32).rearrange(
                    "p (m k x) -> p m k x", m=2, x=2),
                in_=bank[:].rearrange("p (m x k) -> p m k x", m=2, x=2),
            )
            return pin

        def planes(half, pair, pin):
            pc, ps = pcs[half]
            at = slice(256 * pair, 256 * pair + 256)
            nc.vector.quantize_mx(
                out=pc[:, at].bitcast(FP8X4),
                scales=ps[:, at],
                in_=pin[:].rearrange("p k b -> p (k b)"),
            )
            nc.sync.dma_start(
                out=out_1[half].rearrange("p m b -> p (m b)").bitcast(I32)[:, at],
                in_=pc[:, at].bitcast(I32),
            )

        def scales_out(half):
            for x in range(4):
                nc.sync.dma_start(
                    out=out_2[half, 4 * x : 4 * x + 4, :].bitcast(I32),
                    in_=pcs[half][1][32 * x : 32 * x + 4, :].bitcast(I32),
                )

        vcopy = nc.vector.tensor_copy
        scopy = nc.scalar.copy
        for u in range(TAPS):
            for j in range(PACK):
                nc.vector.tensor_scalar(
                    out=diag[:, u, j, :], in0=ident_b[:], scalar1=g1_t[:, u, j : j + 1],
                    scalar2=None, op0=ALU.mult)
        hp = [gain1_pe(768, u) for u in range(3)] + [gain1_pe(512, u) for u in range(4)]

        def qa(hg):
            return quant(hg, 256, "hqa", 256, 8)

        s_a = banks_of("bx")
        v1 = gain1_v(768, 3)
        k0 = qa(hp[0])
        k3 = qa(v1)
        permute_scales()
        permute_words(0)
        mm1(s_a, 256, 256, 0, k0, True, False)
        k1 = qa(hp[1])
        permute_words(1)
        mm1(s_a, 256, 256, 1, k1, False, False)
        permute_words(2)
        k2 = qa(hp[2])
        mm1(s_a, 256, 256, 2, k2, False, False)
        permute_words(3)
        mm1(s_a, 256, 256, 3, k3, False, True)
        mm1(s_a, 0, 256, 0, qa(hp[3]), True, False)
        lay(vcopy, h_int, 1, h_raw, T - 3, T)
        lay(vcopy, h_int, 4, h_raw, 0, 128)
        lay(vcopy, h_int, 4 + 128, h_raw, 128, 256)
        mm1(s_a, 0, 256, 1, qa(hp[4]), False, False)
        lay(vcopy, h_int, 4 + 256, h_raw, 256, 384)
        lay(vcopy, h_int, 4 + 384, h_raw, 384, 512)
        mm1(s_a, 0, 256, 2, qa(hp[5]), False, False)
        mm1(s_a, 0, 256, 3, qa(hp[6]), False, True)
        s_b = banks_of("by")
        hb = [gain1(0), gain1(1)]

        def qb(u):
            q = quant(hb[u], HALF, "hq", HALF, 4)
            mm1(s_b, 0, 512, u, q, u == 0, u == 3)

        for j in range(PACK):
            exp1(1, s_a, j)
        for j in range(PACK):
            ln1(1, j)

        def soft_a(j):
            softplus(1, s_a, j)
            ln2(1, j)

        def soft_b(j):
            softplus(0, s_b, j)
            ln2(0, j)

        qb(0)
        hb.append(gain1(2))
        qb(1)
        hb.append(gain1(3))
        qb(2)
        soft_a(0)
        soft_a(1)
        qb(3)
        soft_a(2)
        soft_a(3)
        lay(vcopy, v_int, 512, v_raw, 512, 768)
        lay(vcopy, v_int, 768, v_raw, 768, 1024)
        nc.vector.tensor_scalar(
            out=mu_b[:], in0=mu_t[:, :, 0], scalar1=-0.5, scalar2=None, op0=ALU.mult
        )
        nc.vector.tensor_copy(out=g2f[:], in_=g2_t[:])
        nc.vector.tensor_scalar(out=ng2f[:], in0=g2_t[:], scalar1=-1.0, scalar2=None, op0=ALU.mult)
        lay(vcopy, v_int, 0, v_raw, 0, 256)
        lay(vcopy, v_int, 256, v_raw, 256, 512)
        rs = [exp2(i) for i in range(4, 8)]
        for j in range(PACK):
            exp1(0, s_b, j)
        for j in range(PACK):
            ln1(0, j)

        def mmq(banks, off, width, u, eg, first=None, last=None):
            mm2(banks, off, width, u, quant(eg, width, "eq", 256, 8), first, last)

        r_a = banks_of("bx")
        ratio(4, rs[0])
        ratio(5, rs[1])
        eg = [pair2(512, 0), pair2(512, 2)]
        pairq(r_a, 0, 0, eg[0])
        ratio(6, rs[2])
        pairq(r_a, 0, 2, eg[1])
        ratio(7, rs[3])
        stage2_unit(r_a, 640, 256, {0: [lambda j=j: soft_b(j) for j in range(4)]})
        rs = [exp2(i) for i in range(4)]
        r_b = banks_of("bx")
        ex_a = {}

        def out_a(m):
            fround(scopy, fmul(ex_a[m], m, HALF, HALF), m, HALF, HALF)

        ratio(0, rs[0])
        ratio(1, rs[1])
        vcopy(out=e_int[:, T : T + 3, :], in_=e_int[:, 0:3, :])
        eg = [pair2(896, 0), pair2(896, 2)]
        s01 = pair2_s(0, 2)
        pairq(r_a, 384, 0, eg[0])
        ratio(2, rs[2])
        pairq(r_a, 384, 2, eg[1])
        ratio(3, rs[3])
        for m in range(4):
            ex_a[m] = fexp(r_a, m, HALF, HALF)
        s3 = gain2_s(128, 256, 3)
        eg = [pair2(0, 0)]
        e = [gain2(128, 256, 0)]
        pairq(r_b, 0, 0, eg[0])
        e.append(gain2(128, 256, 1))
        pairq(r_b, 0, 2, s01)
        out_a(0)
        out_a(1)
        mmq(r_b, 128, 256, 0, e[0])
        out_a(2)
        mmq(r_b, 128, 256, 1, e[1])
        out_a(3)
        e.append(gain2(128, 256, 2))
        mmq(r_b, 128, 256, 3, s3, False, False)
        mmq(r_b, 128, 256, 2, e[2], False, True)
        ex_b = [fexp(r_b, m, 0, 384) for m in range(4)]
        turned = [turn(1, k) for k in range(2)]
        eg = [pair2(384, 0), pair2(384, 2)]
        pairq(r_b, 384, 0, eg[0])
        pairq(r_b, 384, 2, eg[1])
        ex_c = [fexp(r_b, m, 384, 128) for m in range(4)]
        res = [fmul(ex_b[m], m, 0, 384) for m in range(4)]
        for m in range(2):
            fround(scopy, res[m], m, 0, 384)
        pin_a = [pinlay(scopy, turned[k]) for k in range(2)]
        last = [fmul(ex_c[m], m, 384, 128) for m in range(2)]
        for m in range(2):
            fround(vcopy, last[m], m, 384, 128)
        b0 = turn(0, 0)
        last = [fmul(ex_c[m], m, 384, 128) for m in (2, 3)]
        for m in (2, 3):
            fround(vcopy, res[m], m, 0, 384)
        for m in (2, 3):
            fround(vcopy, last[m - 2], m, 384, 128)
        b1 = turn(0, 1)
        p0 = pinlay(scopy, b0)
        for k in range(2):
            planes(1, k, pin_a[k])
        scales_out(1)
        p1 = pinlay(vcopy, b1)
        planes(0, 0, p0)
        planes(0, 1, p1)
        scales_out(0)
